import numpy as np
import ml_dtypes


def mxq(x, axis, fmt="e4m3"):
    dtype, down = {"e4m3": (ml_dtypes.float8_e4m3fn, 7), "e5m2": (ml_dtypes.float8_e5m2, 14)}[fmt]
    v = np.moveaxis(np.asarray(x, np.float32).astype(ml_dtypes.bfloat16).astype(np.float64), axis, -1)
    blocks = v.reshape(v.shape[:-1] + (-1, 32))
    amax = np.abs(blocks).max(-1, keepdims=True)
    byte = np.maximum(np.where(amax > 0, np.frexp(amax)[1] - 1 + 127, 0) - down, 1)
    scale = np.exp2(byte - 127.0)
    codes = (blocks / scale).astype(np.float32).astype(dtype).astype(np.float64)
    return np.moveaxis((codes * scale).reshape(v.shape), -1, axis)


WIDE = False


def mx_kscale(k):
    if not WIDE:
        return np.ones(k)
    levels = np.array([10, -10, 5, -5, 0])
    if k % 512:
        return np.exp2(np.random.permutation(np.resize(levels, k // 32))).repeat(32)
    a = np.empty((k // 512, 16))
    for p in range(k // 512):
        a[p, :8] = np.random.permutation(np.resize(levels, 8))
        for g in range(8):
            far = levels[np.abs(levels - a[p, g]) >= 10]
            a[p, g + 8] = far[np.random.randint(len(far))]
    return np.exp2(a.ravel()).repeat(32)


def f64(x):
    return np.asarray(x).astype(np.float64)


def striped(idx):
    return np.tile(idx.reshape(-1, 16).T, (8, 1)).astype(np.uint16)


def unstriped(offs):
    return offs[:16].T.reshape(-1).astype(np.int64)


E2M1 = np.array([0.0, 0.5, 1.0, 1.5, 2.0, 3.0, 4.0, 6.0, -0.0, -0.5, -1.0, -1.5, -2.0, -3.0, -4.0, -6.0])


def pack_weight(w, fmt):
    k, n = w.shape
    w = f64(np.asarray(w, np.float32).astype(ml_dtypes.bfloat16)).reshape(k // 32, 32, n)
    amax = np.abs(w).max(1)
    if fmt == "e4m3":
        byte = np.frexp(amax)[1] - 1 + 127 - 7
    else:
        mant, ex = np.frexp(amax / 6.0)
        byte = np.where(mant > 0.5, ex, ex - 1) + 127
    byte = np.clip(np.where(amax > 0, byte, 1), 1, 254)
    scaled = (w * np.exp2(127.0 - byte)[:, None, :]).reshape(k, n).astype(np.float32)
    by_word = np.ascontiguousarray(scaled.reshape(k // 512, 128, 4, n).transpose(0, 1, 3, 2))
    if fmt == "e4m3":
        words = by_word.astype(ml_dtypes.float8_e4m3fn).view(np.uint8)
    else:
        c = by_word.astype(ml_dtypes.float4_e2m1fn).view(np.uint8) & 0xF
        words = (c[..., 0::2] | (c[..., 1::2] << 4)).reshape(k // 512, 128, 2 * n)
    return np.ascontiguousarray(words), np.ascontiguousarray(byte.astype(np.uint8).reshape(k // 512, 16, n))


def unpack_weight(words, scales, fmt):
    g, _, n = scales.shape
    words = np.ascontiguousarray(words).reshape(g, 128, n, -1)
    if fmt == "e4m3":
        vals = words.view(ml_dtypes.float8_e4m3fn).astype(np.float64)
    else:
        nib = np.empty((g, 128, n, 4), np.uint8)
        nib[..., 0::2] = words & 0xF
        nib[..., 1::2] = words >> 4
        vals = E2M1[nib]
    vals = vals * np.repeat(np.exp2(scales.astype(np.float64) - 127.0), 8, axis=1)[..., None]
    return vals.transpose(0, 1, 3, 2).reshape(g * 512, n)


K, T, E, C, N = 1024, 768, 24, 128, 256
TOP = 4


def by_expert(wq, xq):
    return np.concatenate([wq[e].T @ xq[:, e * C:(e + 1) * C] for e in range(E)], axis=1)


def setup_inputs():
    n = np.random.standard_normal
    s = mx_kscale(K)[:, None]
    deal = np.repeat(np.arange(E), C).reshape(TOP, T)[:, np.random.permutation(T)]
    deal = np.take_along_axis(deal, np.argsort(np.random.rand(TOP, T), axis=0), axis=0)
    for _ in range(8):
        s_, t_ = np.random.permutation(T).reshape(2, -1); r = np.random.randint(TOP, size=T // 2); x, y = deal[r, s_].copy(), deal[r, t_].copy()
        ok = ~((deal[:, s_] == y).any(0) | (deal[:, t_] == x).any(0)); deal[r[ok], s_[ok]] = y[ok]; deal[r[ok], t_[ok]] = x[ok]
    order = np.lexsort((np.random.rand(TOP * T), deal.reshape(-1)))
    slot_token = order % T; pos = np.empty(TOP * T, np.int64); pos[order] = np.arange(TOP * T); pos = pos.reshape(TOP, T)
    g = np.random.uniform(0.5, 1.5, (TOP, T)); g = g / g.sum(0)
    w = [pack_weight(m, "e2m1") for m in n((E, K, N)) / np.sqrt(K) / s[None]]
    return {
        "xT": (n((K, T)) * s).astype(np.float32),
        "w_words": np.stack([m[0] for m in w]),
        "w_scales": np.stack([m[1] for m in w]),
        "gate": np.stack([np.tile(r, (N, 1)) for r in g]).astype(np.float32),
        "offs": striped(slot_token),
        "pos1": striped(pos[0]),
        "pos2": striped(pos[1]),
        "pos3": striped(pos[2]),
        "pos4": striped(pos[3]),
    }


def reference(xT, w_words, w_scales, gate, offs, pos1, pos2, pos3, pos4):
    idx = unstriped(offs)
    w = np.stack([unpack_weight(w_words[e], w_scales[e], "e2m1") for e in range(E)])
    xq = mxq(f64(xT)[:, idx], 0, "e4m3")
    y = by_expert(w, xq)
    return sum(f64(gate[r]) * y[:, unstriped(p)] for r, p in enumerate((pos1, pos2, pos3, pos4)))

@@ -1,0 +1,198 @@
+from contextlib import ExitStack
+
+import concourse.mybir as mybir
+
+P = 128
+PACK = 4
+K, T, E, C, N = 1024, 768, 24, 128, 256
+TOP = 4
+PASSES = K // (P * PACK)
+HALVES = N // P
+SLOTS = E * C
+FLOPS = 2 * K * N * SLOTS
+
+F32 = mybir.dt.float32
+BF16 = mybir.dt.bfloat16
+I32 = mybir.dt.int32
+U32 = mybir.dt.uint32
+U16 = mybir.dt.uint16
+U8 = mybir.dt.uint8
+FP8X4 = mybir.dt.float8_e4m3fn_x4
+FP4X4 = mybir.dt.float4_e2m1fn_x4
+MULT = mybir.AluOpType.mult
+
+W_BYTES = 2 * N
+GROUP = 4
+CHUNK = GROUP * C
+CHUNKS = SLOTS // CHUNK
+LOADS = (((0, 512), (512, 768)), ((0, 512), (512, 768)))
+
+
+def tile_moe_tk_lin_none_kernel(
+    tc, xT, w_words, w_scales, gate, offs, pos1, pos2, pos3, pos4, out
+):
+    nc = tc.nc
+    with ExitStack() as ctx:
+        lists = ctx.enter_context(tc.tile_pool(name="lists", bufs=1))
+        keep = ctx.enter_context(tc.tile_pool(name="keep", bufs=1))
+        stream = ctx.enter_context(tc.tile_pool(name="stream", bufs=CHUNKS))
+        ring = ctx.enter_context(tc.tile_pool(name="ring", bufs=4))
+        sums = ctx.enter_context(tc.tile_pool(name="sums", bufs=2))
+        psum = ctx.enter_context(tc.psum_pool(name="psum", bufs=6))
+
+        offs_t = lists.tile([P, SLOTS // 16], U16, name="offs_t")
+        pos_t = [lists.tile([P, T // 16], U16, name=f"pos{r}_t") for r in range(TOP)]
+
+        w_sc = keep.tile([P, E * PASSES, N], U8, name="w_sc", align_bytes=64)
+        tok_bytes = keep.tile([P, T], U8, name="tok_bytes", align_bytes=64)
+        slot_bytes = keep.tile([P, SLOTS], U8, name="slot_bytes", align_bytes=64)
+        slot_bytes1 = keep.tile([P, SLOTS], U8, name="slot_bytes1", align_bytes=64)
+        nc.gpsimd.memset(tok_bytes[:].bitcast(I32), 0)
+        nc.vector.memset(w_sc[:].rearrange("p a n -> p (a n)").bitcast(I32), 0)
+        nc.gpsimd.memset(slot_bytes1[:].bitcast(I32), 0)
+
+        x_view = xT.rearrange("(a p j) t -> a p j t", a=PASSES, p=P, j=PACK)
+        raw = {}
+        for a in range(PASSES):
+            for lo, hi in LOADS[a]:
+                tile = keep.tile([P, PACK, hi - lo], F32, name=f"raw{a}_{lo}")
+                nc.sync.dma_start(tile[:], x_view[a][:, :, lo:hi])
+                raw[a, lo] = tile
+            if a == 0:
+                nc.sync.dma_start(offs_t[:], offs)
+
+        s_view = w_scales.bitcast(I32).rearrange("e a q n -> q (e a) n")
+        for q in range(4):
+            nc.sync.dma_start(w_sc[32 * q : 32 * q + 4].bitcast(I32), s_view[4 * q : 4 * q + 4])
+        w_view = w_words.bitcast(I32).rearrange("e a p c -> p (e a) c")
+        w_t = []
+        for g in range(CHUNKS):
+            tile = stream.tile([P, GROUP * PASSES * W_BYTES], U8, name=f"w{g}", tag="stream", align_bytes=64)
+            tile = tile[:].rearrange("p (i c) -> p i c", c=W_BYTES)
+            nc.sync.dma_start(tile.bitcast(I32), w_view[:, g * GROUP * PASSES : (g + 1) * GROUP * PASSES])
+            w_t.append(tile)
+        for r, p in enumerate((pos1, pos2, pos3, pos4)):
+            nc.sync.dma_start(pos_t[r][:], p)
+
+        grouped = [keep.tile([P, T, PACK], BF16, name=f"grouped{a}", align_bytes=64) for a in range(PASSES)]
+        codes = [keep.tile([P, T], U32, name=f"codes{a}", align_bytes=64) for a in range(PASSES)]
+        words = {}
+        y = [keep.tile([P, SLOTS], F32, name=f"y{h}") for h in range(HALVES)]
+
+        def cast(engine_copy, a, load, lo, hi):
+            engine_copy(
+                grouped[a][:, lo:hi, :],
+                raw[a, load][:, :, lo - load : hi - load].rearrange("p j w -> p w j"),
+            )
+
+        def quantise(a, lo, hi):
+            nc.vector.quantize_mx(
+                out=codes[a][:, lo:hi].bitcast(FP8X4),
+                scales=tok_bytes[4 * a : P, lo:hi],
+                in_=grouped[a][:, lo:hi, :].rearrange("p w j -> p (w j)"),
+            )
+
+        def gather_words(a, lo, hi):
+            g = lo // CHUNK
+            if lo == g * CHUNK:
+                words[a, g] = ring.tile([P, CHUNK], U32, name=f"words{a}", align_bytes=64)
+            nc.vector.tensor_copy(
+                words[a, g][:, lo - g * CHUNK : hi - g * CHUNK], codes[a][:].indirect(offs_t[:, lo // 16 : hi // 16])
+            )
+
+        def gather_bytes(lo, hi):
+            nc.vector.tensor_copy(slot_bytes[:, lo:hi], tok_bytes[:].indirect(offs_t[:, lo // 16 : hi // 16]))
+
+        def experts(lo, hi):
+            for h in range(HALVES):
+                bank = psum.tile([P, CHUNK], F32, name="bank")
+                for e in range(lo // C, hi // C):
+                    cols = slice(e * C, (e + 1) * C)
+                    for a in range(PASSES):
+                        i = (e % GROUP) * PASSES + a
+                        nc.tensor.matmul_mx(
+                            out=bank[:, e * C - lo : (e + 1) * C - lo],
+                            lhsT=w_t[e // GROUP][:, i, 2 * P * h : 2 * P * (h + 1)].bitcast(FP4X4),
+                            lhsT_scale=w_sc[:, e * PASSES + a, P * h : P * (h + 1)],
+                            rhs=words[a, e // GROUP][:, (e % GROUP) * C : (e % GROUP + 1) * C].bitcast(FP8X4),
+                            rhs_scale=(slot_bytes1 if a else slot_bytes)[:, cols],
+                            start=(a == 0),
+                            stop=(a == PASSES - 1),
+                        )
+                if h == 0 and hi == SLOTS:
+                    nc.vector.tensor_copy(y[h][:, lo:hi], bank[:, 0 : hi - lo])
+                else:
+                    nc.scalar.copy(y[h][:, lo:hi], bank[:, 0 : hi - lo])
+
+        def gather_group(kind, g):
+            lo, hi = g * CHUNK, (g + 1) * CHUNK
+            if kind == "b":
+                gather_bytes(lo, hi)
+            else:
+                gather_words(kind, lo, hi)
+
+        def shift(lo, hi):
+            nc.gpsimd.dma_start(slot_bytes1[0:112, lo:hi].bitcast(I32), slot_bytes[4:116, lo:hi].bitcast(I32))
+
+        for (lo, hi), cut in zip(LOADS[0], (160, 608)):
+            cast(nc.scalar.copy, 0, lo, lo, cut)
+            cast(nc.vector.tensor_copy, 0, lo, cut, hi)
+            quantise(0, lo, hi)
+        for lo, hi in LOADS[1]:
+            cast(nc.scalar.copy, 1, lo, lo, hi)
+
+        gather_group(0, 0)
+        gather_group(0, 1)
+        gather_group(0, 2)
+        quantise(1, 0, 512)
+        gather_group(0, 3)
+        quantise(1, 512, 768)
+        for g in range(CHUNKS):
+            gather_group("b", g)
+            shift(g * CHUNK, (g + 1) * CHUNK)
+            if g >= 2:
+                gather_group(1, g - 2)
+                experts((g - 2) * CHUNK, (g - 1) * CHUNK)
+        gate_t = []
+        for r in range(TOP):
+            tile = stream.tile([P, HALVES * T], F32, name=f"gate{r}", tag="stream", align_bytes=64)
+            tile = tile[:].rearrange("p (h t) -> p h t", h=HALVES)
+            nc.sync.dma_start(tile, gate[r].rearrange("(h p) t -> p h t", p=P))
+            gate_t.append(tile)
+        gather_group(0, 4)
+        gather_group(1, 4)
+        experts(4 * CHUNK, 5 * CHUNK)
+        gather_group(0, CHUNKS - 1)
+        lo = (CHUNKS - 1) * CHUNK
+        for width in (256, 128, 128):
+            gather_words(1, lo, lo + width)
+            experts(lo, lo + width)
+            lo += width
+
+        def fetch(h, r, tile, lo, hi):
+            nc.vector.tensor_tensor(
+                tile[:, lo:hi], y[h][:].indirect(pos_t[r][:, lo // 16 : hi // 16]), gate_t[r][:, h, lo:hi], MULT
+            )
+
+        def finish(h, prod, part, lo, hi):
+            total = sums.tile([P, T], F32, name="total")
+            nc.vector.tensor_add(total[:, lo:hi], part[:, lo:hi], prod[:, lo:hi])
+            nc.sync.dma_start(out[h * P : (h + 1) * P, lo:hi], total[:, lo:hi])
+
+        left = None
+        for h in range(HALVES):
+            prod = [sums.tile([P, T], F32, name=f"prod{r}") for r in range(TOP)]
+            part = [sums.tile([P, T], F32, name=f"part{s}") for s in range(2)]
+            fetch(h, 0, prod[0], 0, T)
+            fetch(h, 1, prod[1], 0, T)
+            if left:
+                finish(*left)
+            fetch(h, 2, prod[2], 0, T)
+            nc.vector.tensor_add(part[0][:], prod[0][:], prod[1][:])
+            cut = T if h == 0 else 512
+            fetch(h, 3, prod[3], 0, cut)
+            nc.vector.tensor_add(part[1][:], part[0][:], prod[2][:])
+            left = (h, prod[3], part[1], 0, cut)
+        fetch(1, 3, prod[3], 512, T)
+        finish(*left)
+        finish(1, prod[3], part[1], 512, T)

@@ -61,9 +61,9 @@ def tile_moe_tk_lin_none_kernel(
             if a == 0:
                 nc.sync.dma_start(offs_t[:], offs)
 
-        s_view = w_scales.bitcast(I32).rearrange("e a q n -> q (e a) n")
-        for q in range(4):
-            nc.sync.dma_start(w_sc[32 * q : 32 * q + 4].bitcast(I32), s_view[4 * q : 4 * q + 4])
+        s_view = w_scales.bitcast(I32).rearrange("e a (q r) n -> r q (e a) n", r=4)
+        for r in range(4):
+            nc.sync.dma_start(w_sc[r:P:32].bitcast(I32), s_view[r])
         w_view = w_words.bitcast(I32).rearrange("e a p c -> p (e a) c")
         w_t = []
         for g in range(CHUNKS):
@@ -73,6 +73,9 @@ def tile_moe_tk_lin_none_kernel(
             w_t.append(tile)
         for r, p in enumerate((pos1, pos2, pos3, pos4)):
             nc.sync.dma_start(pos_t[r][:], p)
+        gate_t = [keep.tile([P, T], F32, name=f"gate{r}") for r in range(TOP)]
+        for r in range(TOP):
+            nc.sync.dma_start(gate_t[r][:], gate[r, 0:P])
 
         grouped = [keep.tile([P, T, PACK], BF16, name=f"grouped{a}", align_bytes=64) for a in range(PASSES)]
         codes = [keep.tile([P, T], U32, name=f"codes{a}", align_bytes=64) for a in range(PASSES)]
@@ -153,12 +156,6 @@ def tile_moe_tk_lin_none_kernel(
             if g >= 2:
                 gather_group(1, g - 2)
                 experts((g - 2) * CHUNK, (g - 1) * CHUNK)
-        gate_t = []
-        for r in range(TOP):
-            tile = stream.tile([P, HALVES * T], F32, name=f"gate{r}", tag="stream", align_bytes=64)
-            tile = tile[:].rearrange("p (h t) -> p h t", h=HALVES)
-            nc.sync.dma_start(tile, gate[r].rearrange("(h p) t -> p h t", p=P))
-            gate_t.append(tile)
         gather_group(0, 4)
         gather_group(1, 4)
         experts(4 * CHUNK, 5 * CHUNK)
@@ -171,7 +168,7 @@ def tile_moe_tk_lin_none_kernel(
 
         def fetch(h, r, tile, lo, hi):
             nc.vector.tensor_tensor(
-                tile[:, lo:hi], y[h][:].indirect(pos_t[r][:, lo // 16 : hi // 16]), gate_t[r][:, h, lo:hi], MULT
+                tile[:, lo:hi], y[h][:].indirect(pos_t[r][:, lo // 16 : hi // 16]), gate_t[r][:, lo:hi], MULT
             )
 
         def finish(h, prod, part, lo, hi):

@@ -1,6 +1,7 @@
 from contextlib import ExitStack
 
 import concourse.mybir as mybir
+from concourse.masks import make_identity
 
 P = 128
 PACK = 4
@@ -38,7 +39,7 @@ def tile_moe_tk_lin_none_kernel(
         stream = ctx.enter_context(tc.tile_pool(name="stream", bufs=CHUNKS))
         ring = ctx.enter_context(tc.tile_pool(name="ring", bufs=4))
         sums = ctx.enter_context(tc.tile_pool(name="sums", bufs=2))
-        psum = ctx.enter_context(tc.psum_pool(name="psum", bufs=6))
+        psum = ctx.enter_context(tc.psum_pool(name="psum", bufs=8))
 
         offs_t = lists.tile([P, SLOTS // 16], U16, name="offs_t")
         pos_t = [lists.tile([P, T // 16], U16, name=f"pos{r}_t") for r in range(TOP)]
@@ -50,6 +51,8 @@ def tile_moe_tk_lin_none_kernel(
         nc.gpsimd.memset(tok_bytes[:].bitcast(I32), 0)
         nc.vector.memset(w_sc[:].rearrange("p a n -> p (a n)").bitcast(I32), 0)
         nc.gpsimd.memset(slot_bytes1[:].bitcast(I32), 0)
+        ident = keep.tile([P, P], F32, name="ident")
+        make_identity(nc, ident[:])
 
         x_view = xT.rearrange("(a p j) t -> a p j t", a=PASSES, p=P, j=PACK)
         raw = {}
@@ -171,25 +174,74 @@ def tile_moe_tk_lin_none_kernel(
                 tile[:, lo:hi], y[h][:].indirect(pos_t[r][:, lo // 16 : hi // 16]), gate_t[r][:, lo:hi], MULT
             )
 
-        def finish(h, prod, part, lo, hi):
-            total = sums.tile([P, T], F32, name="total")
-            nc.vector.tensor_add(total[:, lo:hi], part[:, lo:hi], prod[:, lo:hi])
-            nc.sync.dma_start(out[h * P : (h + 1) * P, lo:hi], total[:, lo:hi])
+        BANK = T // 2
 
-        left = None
-        for h in range(HALVES):
-            prod = [sums.tile([P, T], F32, name=f"prod{r}") for r in range(TOP)]
-            part = [sums.tile([P, T], F32, name=f"part{s}") for s in range(2)]
-            fetch(h, 0, prod[0], 0, T)
-            fetch(h, 1, prod[1], 0, T)
-            if left:
-                finish(*left)
-            fetch(h, 2, prod[2], 0, T)
-            nc.vector.tensor_add(part[0][:], prod[0][:], prod[1][:])
-            cut = T if h == 0 else 512
-            fetch(h, 3, prod[3], 0, cut)
-            nc.vector.tensor_add(part[1][:], part[0][:], prod[2][:])
-            left = (h, prod[3], part[1], 0, cut)
-        fetch(1, 3, prod[3], 512, T)
-        finish(*left)
-        finish(1, prod[3], part[1], 512, T)
+        turned = {}
+
+        def product(h, r, first, last, by_bank=False):
+            prod = keep.tile([P, T], F32, name=f"prod{h}_{r}")
+            if not by_bank:
+                fetch(h, r, prod, 0, T)
+            for b in range(2):
+                if by_bank:
+                    fetch(h, r, prod, b * BANK, (b + 1) * BANK)
+                if first:
+                    turned[h, b] = psum.tile([P, BANK], F32, name="bank")
+                for c in range(0, BANK, P):
+                    nc.tensor.matmul(
+                        turned[h, b][:, c : c + P],
+                        lhsT=prod[:, b * BANK + c : b * BANK + c + P],
+                        rhs=ident[:],
+                        is_transpose=True,
+                        start=(first and c == 0),
+                        stop=(last and c == BANK - P),
+                    )
+
+        def turn_back(h, b):
+            staged = sums.tile([P, BANK], F32, name="staged")
+            nc.scalar.copy(staged[:], turned[h, b][:])
+            back = psum.tile([P, BANK], F32, name="bank")
+            for c in range(0, BANK, P):
+                nc.tensor.transpose(back[:, c : c + P], staged[:, c : c + P], ident[:])
+            return back
+
+        for r in range(TOP - 1):
+            product(0, r, r == 0, False)
+        product(1, 0, True, False)
+        product(1, 1, False, False)
+        product(0, 3, False, True)
+        for b in range(2):
+            back = turn_back(0, b)
+            total = keep.tile([P, BANK], F32, name=f"total0_{b}")
+            nc.scalar.copy(total[:], back[:])
+            nc.sync.dma_start(out[0:P, b * BANK : (b + 1) * BANK], total[:])
+        product(1, 2, False, True, by_bank=True)
+        backs = [turn_back(1, b) for b in range(2)]
+
+        pieces = ((0, 384), (384, 640), (640, 768))
+        last = []
+
+        def fetch_last(i):
+            lo, hi = pieces[i]
+            prod = sums.tile([P, BANK], F32, name="last")
+            nc.vector.tensor_tensor(
+                prod[:, 0 : hi - lo],
+                y[1][:].indirect(pos_t[TOP - 1][:, lo // 16 : hi // 16]),
+                gate_t[TOP - 1][:, lo:hi],
+                MULT,
+            )
+            last.append(prod)
+
+        def finish(i):
+            lo, hi = pieces[i]
+            b = lo // BANK
+            total = keep.tile([P, hi - lo], F32, name=f"total1_{i}")
+            nc.vector.tensor_add(total[:], backs[b][:, lo - b * BANK : hi - b * BANK], last[i][:, 0 : hi - lo])
+            nc.sync.dma_start(out[P : 2 * P, lo:hi], total[:])
+
+        fetch_last(0)
+        fetch_last(1)
+        finish(0)
+        fetch_last(2)
+        finish(1)
+        finish(2)

@@ -39,7 +39,8 @@ def tile_moe_tk_lin_none_kernel(
         stream = ctx.enter_context(tc.tile_pool(name="stream", bufs=CHUNKS))
         ring = ctx.enter_context(tc.tile_pool(name="ring", bufs=4))
         sums = ctx.enter_context(tc.tile_pool(name="sums", bufs=2))
-        psum = ctx.enter_context(tc.psum_pool(name="psum", bufs=8))
+        psum = ctx.enter_context(tc.psum_pool(name="psum", bufs=6))
+        turns = ctx.enter_context(tc.psum_pool(name="turns", bufs=2))
 
         offs_t = lists.tile([P, SLOTS // 16], U16, name="offs_t")
         pos_t = [lists.tile([P, T // 16], U16, name=f"pos{r}_t") for r in range(TOP)]
@@ -87,8 +88,8 @@ def tile_moe_tk_lin_none_kernel(
 
         def cast(engine_copy, a, load, lo, hi):
             engine_copy(
-                grouped[a][:, lo:hi, :],
-                raw[a, load][:, :, lo - load : hi - load].rearrange("p j w -> p w j"),
+                grouped[a][:, lo:hi, :].rearrange("p (c i) j -> p c j i", i=PACK),
+                raw[a, load][:, :, lo - load : hi - load].rearrange("p j (c i) -> p c j i", i=PACK),
             )
 
         def quantise(a, lo, hi):
@@ -178,24 +179,25 @@ def tile_moe_tk_lin_none_kernel(
 
         turned = {}
 
-        def product(h, r, first, last, by_bank=False):
-            prod = keep.tile([P, T], F32, name=f"prod{h}_{r}")
-            if not by_bank:
-                fetch(h, r, prod, 0, T)
-            for b in range(2):
-                if by_bank:
-                    fetch(h, r, prod, b * BANK, (b + 1) * BANK)
-                if first:
-                    turned[h, b] = psum.tile([P, BANK], F32, name="bank")
-                for c in range(0, BANK, P):
-                    nc.tensor.matmul(
-                        turned[h, b][:, c : c + P],
-                        lhsT=prod[:, b * BANK + c : b * BANK + c + P],
-                        rhs=ident[:],
-                        is_transpose=True,
-                        start=(first and c == 0),
-                        stop=(last and c == BANK - P),
-                    )
+        prods = {}
+
+        def product(h, r, lo=0, hi=T):
+            if lo == 0:
+                prods[h, r] = keep.tile([P, T], F32, name=f"prod{h}_{r}")
+            fetch(h, r, prods[h, r], lo, hi)
+
+        def turn(h, r, b, last):
+            if r == 0:
+                turned[h, b] = turns.tile([P, BANK], F32, name="turned")
+            for c in range(0, BANK, P):
+                nc.tensor.matmul(
+                    turned[h, b][:, c : c + P],
+                    lhsT=prods[h, r][:, b * BANK + c : b * BANK + c + P],
+                    rhs=ident[:],
+                    is_transpose=True,
+                    start=(r == 0 and c == 0),
+                    stop=(r == last and c == BANK - P),
+                )
 
         def turn_back(h, b):
             staged = sums.tile([P, BANK], F32, name="staged")
@@ -205,17 +207,24 @@ def tile_moe_tk_lin_none_kernel(
                 nc.tensor.transpose(back[:, c : c + P], staged[:, c : c + P], ident[:])
             return back
 
-        for r in range(TOP - 1):
-            product(0, r, r == 0, False)
-        product(1, 0, True, False)
-        product(1, 1, False, False)
-        product(0, 3, False, True)
+        for r in range(TOP):
+            if r == TOP - 1:
+                product(1, 0)
+            product(0, r)
+            for b in range(2):
+                turn(0, r, b, TOP - 1)
         for b in range(2):
             back = turn_back(0, b)
             total = keep.tile([P, BANK], F32, name=f"total0_{b}")
             nc.scalar.copy(total[:], back[:])
             nc.sync.dma_start(out[0:P, b * BANK : (b + 1) * BANK], total[:])
-        product(1, 2, False, True, by_bank=True)
+        product(1, 1)
+        for r in range(2):
+            for b in range(2):
+                turn(1, r, b, TOP - 2)
+        for b in range(2):
+            product(1, 2, b * BANK, (b + 1) * BANK)
+            turn(1, 2, b, TOP - 2)
         backs = [turn_back(1, b) for b in range(2)]
 
         pieces = ((0, 384), (384, 640), (640, 768))

@@ -110,8 +110,8 @@ def tile_moe_tk_lin_none_kernel(
         def gather_bytes(lo, hi):
             nc.vector.tensor_copy(slot_bytes[:, lo:hi], tok_bytes[:].indirect(offs_t[:, lo // 16 : hi // 16]))
 
-        def experts(lo, hi):
-            for h in range(HALVES):
+        def experts(lo, hi, halves=range(HALVES)):
+            for h in halves:
                 bank = psum.tile([P, CHUNK], F32, name="bank")
                 for e in range(lo // C, hi // C):
                     cols = slice(e * C, (e + 1) * C)
@@ -167,8 +167,9 @@ def tile_moe_tk_lin_none_kernel(
         lo = (CHUNKS - 1) * CHUNK
         for width in (256, 128, 128):
             gather_words(1, lo, lo + width)
-            experts(lo, lo + width)
+            experts(lo, lo + width, (0,))
             lo += width
+        experts((CHUNKS - 1) * CHUNK, SLOTS, (1,))
 
         def fetch(h, r, tile, lo, hi):
             nc.vector.tensor_tensor(
@@ -208,8 +209,6 @@ def tile_moe_tk_lin_none_kernel(
             return back
 
         for r in range(TOP):
-            if r == TOP - 1:
-                product(1, 0)
             product(0, r)
             for b in range(2):
                 turn(0, r, b, TOP - 1)
@@ -218,8 +217,8 @@ def tile_moe_tk_lin_none_kernel(
             total = keep.tile([P, BANK], F32, name=f"total0_{b}")
             nc.scalar.copy(total[:], back[:])
             nc.sync.dma_start(out[0:P, b * BANK : (b + 1) * BANK], total[:])
-        product(1, 1)
         for r in range(2):
+            product(1, r)
             for b in range(2):
                 turn(1, r, b, TOP - 2)
         for b in range(2):

@@ -26,7 +26,7 @@ W_BYTES = 2 * N
 GROUP = 4
 CHUNK = GROUP * C
 CHUNKS = SLOTS // CHUNK
-LOADS = (((0, 512), (512, 768)), ((0, 512), (512, 768)))
+LOADS = (((0, 384), (384, 640), (640, 768)), ((0, 256), (256, 512), (512, 768)))
 
 
 def tile_moe_tk_lin_none_kernel(
@@ -64,6 +64,7 @@ def tile_moe_tk_lin_none_kernel(
                 raw[a, lo] = tile
             if a == 0:
                 nc.sync.dma_start(offs_t[:], offs)
+        nc.sync.dma_start(pos_t[0][:], pos1)
 
         s_view = w_scales.bitcast(I32).rearrange("e a (q r) n -> r q (e a) n", r=4)
         for r in range(4):
@@ -75,8 +76,8 @@ def tile_moe_tk_lin_none_kernel(
             tile = tile[:].rearrange("p (i c) -> p i c", c=W_BYTES)
             nc.sync.dma_start(tile.bitcast(I32), w_view[:, g * GROUP * PASSES : (g + 1) * GROUP * PASSES])
             w_t.append(tile)
-        for r, p in enumerate((pos1, pos2, pos3, pos4)):
-            nc.sync.dma_start(pos_t[r][:], p)
+        for r, p in enumerate((pos2, pos3, pos4)):
+            nc.sync.dma_start(pos_t[r + 1][:], p)
         gate_t = [keep.tile([P, T], F32, name=f"gate{r}") for r in range(TOP)]
         for r in range(TOP):
             nc.sync.dma_start(gate_t[r][:], gate[r, 0:P])
@@ -141,10 +142,14 @@ def tile_moe_tk_lin_none_kernel(
         def shift(lo, hi):
             nc.gpsimd.dma_start(slot_bytes1[0:112, lo:hi].bitcast(I32), slot_bytes[4:116, lo:hi].bitcast(I32))
 
-        for (lo, hi), cut in zip(LOADS[0], (160, 608)):
+        for (lo, hi), cut in zip(LOADS[0], (128, 512, 736)):
             cast(nc.scalar.copy, 0, lo, lo, cut)
             cast(nc.vector.tensor_copy, 0, lo, cut, hi)
-            quantise(0, lo, hi)
+            if lo == 0:
+                quantise(0, cut, hi)
+                quantise(0, lo, cut)
+            else:
+                quantise(0, lo, hi)
         for lo, hi in LOADS[1]:
             cast(nc.scalar.copy, 1, lo, lo, hi)
 
@@ -152,8 +157,8 @@ def tile_moe_tk_lin_none_kernel(
         gather_group(0, 1)
         gather_group(0, 2)
         quantise(1, 0, 512)
-        gather_group(0, 3)
         quantise(1, 512, 768)
+        gather_group(0, 3)
         for g in range(CHUNKS):
             gather_group("b", g)
             shift(g * CHUNK, (g + 1) * CHUNK)

@@ -39,7 +39,7 @@ def tile_moe_tk_lin_none_kernel(
         stream = ctx.enter_context(tc.tile_pool(name="stream", bufs=CHUNKS))
         ring = ctx.enter_context(tc.tile_pool(name="ring", bufs=4))
         sums = ctx.enter_context(tc.tile_pool(name="sums", bufs=2))
-        psum = ctx.enter_context(tc.psum_pool(name="psum", bufs=6))
+        psum = ctx.enter_context(tc.psum_pool(name="psum", bufs=1))
         turns = ctx.enter_context(tc.psum_pool(name="turns", bufs=2))
 
         offs_t = lists.tile([P, SLOTS // 16], U16, name="offs_t")
@@ -111,10 +111,17 @@ def tile_moe_tk_lin_none_kernel(
         def gather_bytes(lo, hi):
             nc.vector.tensor_copy(slot_bytes[:, lo:hi], tok_bytes[:].indirect(offs_t[:, lo // 16 : hi // 16]))
 
-        def experts(lo, hi, halves=range(HALVES)):
+        banks = [psum.tile([P, CHUNK], F32, name=f"bank{i}") for i in range(6)]
+        turn_of = [0]
+
+        def next_bank():
+            turn_of[0] = turn_of[0] + 1
+            return banks[(turn_of[0] - 1) % 6]
+
+        def experts(lo, hi, halves=range(HALVES), held=None, step=1):
             for h in halves:
-                bank = psum.tile([P, CHUNK], F32, name="bank")
-                for e in range(lo // C, hi // C):
+                bank = next_bank() if held is None else held
+                for e in range(lo // C, hi // C)[::step]:
                     cols = slice(e * C, (e + 1) * C)
                     for a in range(PASSES):
                         i = (e % GROUP) * PASSES + a
@@ -162,9 +169,12 @@ def tile_moe_tk_lin_none_kernel(
         for g in range(CHUNKS):
             gather_group("b", g)
             shift(g * CHUNK, (g + 1) * CHUNK)
-            if g >= 2:
-                gather_group(1, g - 2)
-                experts((g - 2) * CHUNK, (g - 1) * CHUNK)
+            if g == 3:
+                gather_group(1, 0)
+                experts(0, CHUNK)
+        for g in range(1, 4):
+            gather_group(1, g)
+            experts(g * CHUNK, (g + 1) * CHUNK, range(HALVES) if g < 3 else (0,))
         gather_group(0, 4)
         gather_group(1, 4)
         experts(4 * CHUNK, 5 * CHUNK)
@@ -174,7 +184,8 @@ def tile_moe_tk_lin_none_kernel(
             gather_words(1, lo, lo + width)
             experts(lo, lo + width, (0,))
             lo += width
-        experts((CHUNKS - 1) * CHUNK, SLOTS, (1,))
+        experts(5 * CHUNK, 6 * CHUNK, (1,), banks[0], -1)
+        experts(3 * CHUNK, 4 * CHUNK, (1,), banks[5])
 
         def fetch(h, r, tile, lo, hi):
             nc.vector.tensor_tensor(
@@ -208,7 +219,7 @@ def tile_moe_tk_lin_none_kernel(
         def turn_back(h, b):
             staged = sums.tile([P, BANK], F32, name="staged")
             nc.scalar.copy(staged[:], turned[h, b][:])
-            back = psum.tile([P, BANK], F32, name="bank")
+            back = banks[2 * h + b][:, 0:BANK]
             for c in range(0, BANK, P):
                 nc.tensor.transpose(back[:, c : c + P], staged[:, c : c + P], ident[:])
             return back

@@ -64,11 +64,16 @@ def tile_moe_tk_lin_none_kernel(
                 raw[a, lo] = tile
             if a == 0:
                 nc.sync.dma_start(offs_t[:], offs)
-        nc.sync.dma_start(pos_t[0][:], pos1)
+                landed = keep.tile([P, E * PASSES * N], U8, name="landed", align_bytes=64)
+                nc.sync.dma_start(
+                    landed[4:P:8].bitcast(I32).rearrange("q (i n) -> q i n", i=E * PASSES),
+                    w_scales.bitcast(I32).rearrange("e a q n -> q (e a) n"),
+                )
 
-        s_view = w_scales.bitcast(I32).rearrange("e a (q r) n -> r q (e a) n", r=4)
         for r in range(4):
-            nc.sync.dma_start(w_sc[r:P:32].bitcast(I32), s_view[r])
+            nc.gpsimd.dma_start(
+                w_sc[r:P:32].rearrange("q i n -> q (i n)").bitcast(I32), landed[4 + 8 * r : P : 32].bitcast(I32)
+            )
         w_view = w_words.bitcast(I32).rearrange("e a p c -> p (e a) c")
         w_t = []
         for g in range(CHUNKS):
@@ -76,8 +81,8 @@ def tile_moe_tk_lin_none_kernel(
             tile = tile[:].rearrange("p (i c) -> p i c", c=W_BYTES)
             nc.sync.dma_start(tile.bitcast(I32), w_view[:, g * GROUP * PASSES : (g + 1) * GROUP * PASSES])
             w_t.append(tile)
-        for r, p in enumerate((pos2, pos3, pos4)):
-            nc.sync.dma_start(pos_t[r + 1][:], p)
+        for r, p in enumerate((pos1, pos2, pos3, pos4)):
+            nc.sync.dma_start(pos_t[r][:], p)
         gate_t = [keep.tile([P, T], F32, name=f"gate{r}") for r in range(TOP)]
         for r in range(TOP):
             nc.sync.dma_start(gate_t[r][:], gate[r, 0:P])

@@ -139,10 +139,7 @@ def tile_moe_tk_lin_none_kernel(
                             start=(a == 0),
                             stop=(a == PASSES - 1),
                         )
-                if h == 0 and hi == SLOTS:
-                    nc.vector.tensor_copy(y[h][:, lo:hi], bank[:, 0 : hi - lo])
-                else:
-                    nc.scalar.copy(y[h][:, lo:hi], bank[:, 0 : hi - lo])
+                nc.scalar.copy(y[h][:, lo:hi], bank[:, 0 : hi - lo])
 
         def gather_group(kind, g):
             lo, hi = g * CHUNK, (g + 1) * CHUNK
@@ -168,9 +165,9 @@ def tile_moe_tk_lin_none_kernel(
         gather_group(0, 0)
         gather_group(0, 1)
         gather_group(0, 2)
+        gather_group(0, 3)
         quantise(1, 0, 512)
         quantise(1, 512, 768)
-        gather_group(0, 3)
         for g in range(CHUNKS):
             gather_group("b", g)
             shift(g * CHUNK, (g + 1) * CHUNK)

@@ -37,7 +37,7 @@ def tile_moe_tk_lin_none_kernel(
         lists = ctx.enter_context(tc.tile_pool(name="lists", bufs=1))
         keep = ctx.enter_context(tc.tile_pool(name="keep", bufs=1))
         stream = ctx.enter_context(tc.tile_pool(name="stream", bufs=CHUNKS))
-        ring = ctx.enter_context(tc.tile_pool(name="ring", bufs=4))
+        ring = ctx.enter_context(tc.tile_pool(name="ring", bufs=5))
         sums = ctx.enter_context(tc.tile_pool(name="sums", bufs=2))
         psum = ctx.enter_context(tc.psum_pool(name="psum", bufs=1))
         turns = ctx.enter_context(tc.psum_pool(name="turns", bufs=2))
@@ -168,6 +168,7 @@ def tile_moe_tk_lin_none_kernel(
         gather_group(0, 3)
         quantise(1, 0, 512)
         quantise(1, 512, 768)
+        gather_group(0, 4)
         for g in range(CHUNKS):
             gather_group("b", g)
             shift(g * CHUNK, (g + 1) * CHUNK)
@@ -177,7 +178,6 @@ def tile_moe_tk_lin_none_kernel(
         for g in range(1, 4):
             gather_group(1, g)
             experts(g * CHUNK, (g + 1) * CHUNK, range(HALVES) if g < 3 else (0,))
-        gather_group(0, 4)
         gather_group(1, 4)
         experts(4 * CHUNK, 5 * CHUNK)
         gather_group(0, CHUNKS - 1)
@@ -194,10 +194,9 @@ def tile_moe_tk_lin_none_kernel(
                 tile[:, lo:hi], y[h][:].indirect(pos_t[r][:, lo // 16 : hi // 16]), gate_t[r][:, lo:hi], MULT
             )
 
-        BANK = T // 2
-
-        turned = {}
-
+        BLOCKS = (((0, 512), (512, 768)), ((0, 384), (384, 768)))
+        turned = {(1, 0): banks[1], (1, 1): banks[2]}
+        back_bank = {(1, 0): banks[3], (1, 1): banks[4], (0, 0): banks[0], (0, 1): banks[5]}
         prods = {}
 
         def product(h, r, lo=0, hi=T):
@@ -206,44 +205,55 @@ def tile_moe_tk_lin_none_kernel(
             fetch(h, r, prods[h, r], lo, hi)
 
         def turn(h, r, b, last):
-            if r == 0:
-                turned[h, b] = turns.tile([P, BANK], F32, name="turned")
-            for c in range(0, BANK, P):
+            lo, hi = BLOCKS[h][b]
+            if (h, b) not in turned:
+                turned[h, b] = turns.tile([P, CHUNK], F32, name="turned")
+            for c in range(lo, hi, P):
                 nc.tensor.matmul(
-                    turned[h, b][:, c : c + P],
-                    lhsT=prods[h, r][:, b * BANK + c : b * BANK + c + P],
+                    turned[h, b][:, c - lo : c - lo + P],
+                    lhsT=prods[h, r][:, c : c + P],
                     rhs=ident[:],
                     is_transpose=True,
-                    start=(r == 0 and c == 0),
-                    stop=(r == last and c == BANK - P),
+                    start=(r == 0 and c == lo),
+                    stop=(r == last and c == hi - P),
                 )
 
         def turn_back(h, b):
-            staged = sums.tile([P, BANK], F32, name="staged")
-            nc.scalar.copy(staged[:], turned[h, b][:])
-            back = banks[2 * h + b][:, 0:BANK]
-            for c in range(0, BANK, P):
+            lo, hi = BLOCKS[h][b]
+            staged = keep.tile([P, hi - lo], F32, name=f"staged{h}_{b}")
+            nc.scalar.copy(staged[:], turned[h, b][:, 0 : hi - lo])
+            back = back_bank[h, b][:, 0 : hi - lo]
+            for c in range(0, hi - lo, P):
                 nc.tensor.transpose(back[:, c : c + P], staged[:, c : c + P], ident[:])
             return back
 
-        for r in range(TOP):
-            product(0, r)
+        def whole(h, r):
+            product(h, r)
             for b in range(2):
-                turn(0, r, b, TOP - 1)
-        for b in range(2):
-            back = turn_back(0, b)
-            total = keep.tile([P, BANK], F32, name=f"total0_{b}")
-            nc.scalar.copy(total[:], back[:])
-            nc.sync.dma_start(out[0:P, b * BANK : (b + 1) * BANK], total[:])
-        for r in range(2):
-            product(1, r)
-            for b in range(2):
-                turn(1, r, b, TOP - 2)
-        for b in range(2):
-            product(1, 2, b * BANK, (b + 1) * BANK)
-            turn(1, 2, b, TOP - 2)
-        backs = [turn_back(1, b) for b in range(2)]
+                turn(h, r, b, TOP - 1 - h)
 
+        def close_first_half(b):
+            lo, hi = BLOCKS[0][b]
+            product(0, TOP - 1, lo, hi)
+            turn(0, TOP - 1, b, TOP - 1)
+            back = turn_back(0, b)
+            total = keep.tile([P, hi - lo], F32, name=f"total0_{b}")
+            nc.scalar.copy(total[:], back[:])
+            nc.sync.dma_start(out[0:P, lo:hi], total[:])
+
+        for r in range(TOP - 1):
+            whole(0, r)
+        whole(1, 0)
+        close_first_half(0)
+        whole(1, 1)
+        backs = []
+        for b, (lo, hi) in enumerate(BLOCKS[1]):
+            product(1, 2, lo, hi)
+            turn(1, 2, b, 2)
+            backs.append(turn_back(1, b))
+        close_first_half(1)
+
+        BANK = T // 2
         pieces = ((0, 384), (384, 640), (640, 768))
         last = []
 

@@ -38,7 +38,6 @@ def tile_moe_tk_lin_none_kernel(
         keep = ctx.enter_context(tc.tile_pool(name="keep", bufs=1))
         stream = ctx.enter_context(tc.tile_pool(name="stream", bufs=CHUNKS))
         ring = ctx.enter_context(tc.tile_pool(name="ring", bufs=5))
-        sums = ctx.enter_context(tc.tile_pool(name="sums", bufs=2))
         psum = ctx.enter_context(tc.psum_pool(name="psum", bufs=1))
         turns = ctx.enter_context(tc.psum_pool(name="turns", bufs=2))
 
@@ -194,9 +193,8 @@ def tile_moe_tk_lin_none_kernel(
                 tile[:, lo:hi], y[h][:].indirect(pos_t[r][:, lo // 16 : hi // 16]), gate_t[r][:, lo:hi], MULT
             )
 
-        BLOCKS = (((0, 512), (512, 768)), ((0, 384), (384, 768)))
-        turned = {(1, 0): banks[1], (1, 1): banks[2]}
-        back_bank = {(1, 0): banks[3], (1, 1): banks[4], (0, 0): banks[0], (0, 1): banks[5]}
+        BLOCKS = (((0, 384), (384, 768)), ((0, 256), (256, 512), (512, 768)))
+        turned = {(1, b): banks[2 + b] for b in range(3)}
         prods = {}
 
         def product(h, r, lo=0, hi=T):
@@ -204,7 +202,7 @@ def tile_moe_tk_lin_none_kernel(
                 prods[h, r] = keep.tile([P, T], F32, name=f"prod{h}_{r}")
             fetch(h, r, prods[h, r], lo, hi)
 
-        def turn(h, r, b, last):
+        def turn(h, r, b):
             lo, hi = BLOCKS[h][b]
             if (h, b) not in turned:
                 turned[h, b] = turns.tile([P, CHUNK], F32, name="turned")
@@ -215,69 +213,48 @@ def tile_moe_tk_lin_none_kernel(
                     rhs=ident[:],
                     is_transpose=True,
                     start=(r == 0 and c == lo),
-                    stop=(r == last and c == hi - P),
+                    stop=(r == TOP - 1 - h and c == hi - P),
                 )
 
-        def turn_back(h, b):
+        def turn_back(h, b, bank):
             lo, hi = BLOCKS[h][b]
             staged = keep.tile([P, hi - lo], F32, name=f"staged{h}_{b}")
             nc.scalar.copy(staged[:], turned[h, b][:, 0 : hi - lo])
-            back = back_bank[h, b][:, 0 : hi - lo]
             for c in range(0, hi - lo, P):
-                nc.tensor.transpose(back[:, c : c + P], staged[:, c : c + P], ident[:])
-            return back
+                nc.tensor.transpose(bank[:, c : c + P], staged[:, c : c + P], ident[:])
+            return bank[:, 0 : hi - lo]
 
         def whole(h, r):
             product(h, r)
-            for b in range(2):
-                turn(h, r, b, TOP - 1 - h)
+            for b in range(len(BLOCKS[h])):
+                turn(h, r, b)
 
-        def close_first_half(b):
-            lo, hi = BLOCKS[0][b]
-            product(0, TOP - 1, lo, hi)
-            turn(0, TOP - 1, b, TOP - 1)
-            back = turn_back(0, b)
-            total = keep.tile([P, hi - lo], F32, name=f"total0_{b}")
-            nc.scalar.copy(total[:], back[:])
-            nc.sync.dma_start(out[0:P, lo:hi], total[:])
-
-        for r in range(TOP - 1):
+        for r in range(TOP):
             whole(0, r)
+        for b, (lo, hi) in enumerate(BLOCKS[0]):
+            back = turn_back(0, b, banks[b])
+            total = keep.tile([P, hi - lo], F32, name=f"total0_{b}")
+            nc.scalar.copy(total[:], back)
+            nc.sync.dma_start(out[0:P, lo:hi], total[:])
         whole(1, 0)
-        close_first_half(0)
         whole(1, 1)
         backs = []
         for b, (lo, hi) in enumerate(BLOCKS[1]):
             product(1, 2, lo, hi)
-            turn(1, 2, b, 2)
-            backs.append(turn_back(1, b))
-        close_first_half(1)
+            turn(1, 2, b)
+            backs.append(turn_back(1, b, banks[(5 + b) % 6]))
 
-        BANK = T // 2
-        pieces = ((0, 384), (384, 640), (640, 768))
-        last = []
+        last = keep.tile([P, T], F32, name="last")
 
-        def fetch_last(i):
-            lo, hi = pieces[i]
-            prod = sums.tile([P, BANK], F32, name="last")
-            nc.vector.tensor_tensor(
-                prod[:, 0 : hi - lo],
-                y[1][:].indirect(pos_t[TOP - 1][:, lo // 16 : hi // 16]),
-                gate_t[TOP - 1][:, lo:hi],
-                MULT,
-            )
-            last.append(prod)
-
-        def finish(i):
-            lo, hi = pieces[i]
-            b = lo // BANK
-            total = keep.tile([P, hi - lo], F32, name=f"total1_{i}")
-            nc.vector.tensor_add(total[:], backs[b][:, lo - b * BANK : hi - b * BANK], last[i][:, 0 : hi - lo])
+        def finish(lo, hi):
+            b = lo // 256
+            total = keep.tile([P, hi - lo], F32, name=f"total1_{lo}")
+            nc.vector.tensor_add(total[:], backs[b][:, lo - 256 * b : hi - 256 * b], last[:, lo:hi])
             nc.sync.dma_start(out[P : 2 * P, lo:hi], total[:])
 
-        fetch_last(0)
-        fetch_last(1)
-        finish(0)
-        fetch_last(2)
-        finish(1)
-        finish(2)
+        fetch(1, TOP - 1, last, 0, 256)
+        fetch(1, TOP - 1, last, 256, 512)
+        finish(0, 256)
+        fetch(1, TOP - 1, last, 512, 768)
+        finish(256, 512)
+        finish(512, 768)

@@ -37,7 +37,7 @@ def tile_moe_tk_lin_none_kernel(
         lists = ctx.enter_context(tc.tile_pool(name="lists", bufs=1))
         keep = ctx.enter_context(tc.tile_pool(name="keep", bufs=1))
         stream = ctx.enter_context(tc.tile_pool(name="stream", bufs=CHUNKS))
-        ring = ctx.enter_context(tc.tile_pool(name="ring", bufs=5))
+        ring = ctx.enter_context(tc.tile_pool(name="ring", bufs=4))
         psum = ctx.enter_context(tc.psum_pool(name="psum", bufs=1))
         turns = ctx.enter_context(tc.psum_pool(name="turns", bufs=2))
 
@@ -161,24 +161,19 @@ def tile_moe_tk_lin_none_kernel(
         for lo, hi in LOADS[1]:
             cast(nc.scalar.copy, 1, lo, lo, hi)
 
-        gather_group(0, 0)
-        gather_group(0, 1)
-        gather_group(0, 2)
-        gather_group(0, 3)
+        for g in range(4):
+            gather_group(0, g)
         quantise(1, 0, 512)
         quantise(1, 512, 768)
-        gather_group(0, 4)
         for g in range(CHUNKS):
             gather_group("b", g)
             shift(g * CHUNK, (g + 1) * CHUNK)
-            if g == 3:
-                gather_group(1, 0)
-                experts(0, CHUNK)
-        for g in range(1, 4):
-            gather_group(1, g)
-            experts(g * CHUNK, (g + 1) * CHUNK, range(HALVES) if g < 3 else (0,))
+            if g >= 2:
+                gather_group(1, g - 2)
+                experts((g - 2) * CHUNK, (g - 1) * CHUNK)
+        gather_group(0, 4)
         gather_group(1, 4)
-        experts(4 * CHUNK, 5 * CHUNK)
+        experts(4 * CHUNK, 5 * CHUNK, (0,))
         gather_group(0, CHUNKS - 1)
         lo = (CHUNKS - 1) * CHUNK
         for width in (256, 128, 128):
@@ -186,7 +181,7 @@ def tile_moe_tk_lin_none_kernel(
             experts(lo, lo + width, (0,))
             lo += width
         experts(5 * CHUNK, 6 * CHUNK, (1,), banks[0], -1)
-        experts(3 * CHUNK, 4 * CHUNK, (1,), banks[5])
+        experts(4 * CHUNK, 5 * CHUNK, (1,), banks[5])
 
         def fetch(h, r, tile, lo, hi):
             nc.vector.tensor_tensor(

@@ -188,7 +188,7 @@ def tile_moe_tk_lin_none_kernel(
                 tile[:, lo:hi], y[h][:].indirect(pos_t[r][:, lo // 16 : hi // 16]), gate_t[r][:, lo:hi], MULT
             )
 
-        BLOCKS = (((0, 384), (384, 768)), ((0, 256), (256, 512), (512, 768)))
+        BLOCKS = (((0, 512), (512, 768)), ((0, 256), (256, 512), (512, 768)))
         turned = {(1, b): banks[2 + b] for b in range(3)}
         prods = {}
 
@@ -208,7 +208,7 @@ def tile_moe_tk_lin_none_kernel(
                     rhs=ident[:],
                     is_transpose=True,
                     start=(r == 0 and c == lo),
-                    stop=(r == TOP - 1 - h and c == hi - P),
+                    stop=(r == (TOP - 1 if (h, b) == (0, 0) else TOP - 2) and c == hi - P),
                 )
 
         def turn_back(h, b, bank):
@@ -224,32 +224,36 @@ def tile_moe_tk_lin_none_kernel(
             for b in range(len(BLOCKS[h])):
                 turn(h, r, b)
 
-        for r in range(TOP):
+        for r in range(TOP - 1):
             whole(0, r)
-        for b, (lo, hi) in enumerate(BLOCKS[0]):
-            back = turn_back(0, b, banks[b])
-            total = keep.tile([P, hi - lo], F32, name=f"total0_{b}")
-            nc.scalar.copy(total[:], back)
-            nc.sync.dma_start(out[0:P, lo:hi], total[:])
+        backs = {(0, 1): turn_back(0, 1, banks[1])}
         whole(1, 0)
+        product(0, TOP - 1, 0, 512)
+        turn(0, TOP - 1, 0)
+        back = turn_back(0, 0, banks[0])
+        total = keep.tile([P, 512], F32, name="total0_0")
+        nc.scalar.copy(total[:], back)
+        nc.sync.dma_start(out[0:P, 0:512], total[:])
         whole(1, 1)
-        backs = []
+        spare = turns.tile([P, CHUNK], F32, name="turned")
         for b, (lo, hi) in enumerate(BLOCKS[1]):
             product(1, 2, lo, hi)
             turn(1, 2, b)
-            backs.append(turn_back(1, b, banks[(5 + b) % 6]))
+            backs[1, b] = turn_back(1, b, (banks[5], spare, banks[0])[b])
 
         last = keep.tile([P, T], F32, name="last")
 
-        def finish(lo, hi):
-            b = lo // 256
-            total = keep.tile([P, hi - lo], F32, name=f"total1_{lo}")
-            nc.vector.tensor_add(total[:], backs[b][:, lo - 256 * b : hi - 256 * b], last[:, lo:hi])
-            nc.sync.dma_start(out[P : 2 * P, lo:hi], total[:])
+        def finish(h, b, prod):
+            lo, hi = BLOCKS[h][b]
+            total = keep.tile([P, hi - lo], F32, name=f"total{h}_{b}")
+            nc.vector.tensor_add(total[:], backs[h, b], prod[:, lo:hi])
+            nc.sync.dma_start(out[h * P : (h + 1) * P, lo:hi], total[:])
 
+        product(0, TOP - 1, 512, 768)
         fetch(1, TOP - 1, last, 0, 256)
+        finish(0, 1, prods[0, TOP - 1])
         fetch(1, TOP - 1, last, 256, 512)
-        finish(0, 256)
+        finish(1, 0, last)
         fetch(1, TOP - 1, last, 512, 768)
-        finish(256, 512)
-        finish(512, 768)
+        finish(1, 1, last)
+        finish(1, 2, last)

@@ -122,22 +122,24 @@ def tile_moe_tk_lin_none_kernel(
             turn_of[0] = turn_of[0] + 1
             return banks[(turn_of[0] - 1) % 6]
 
-        def experts(lo, hi, halves=range(HALVES), held=None, step=1):
+        def one_pass(e, h, a, target):
+            i = (e % GROUP) * PASSES + a
+            nc.tensor.matmul_mx(
+                out=target,
+                lhsT=w_t[e // GROUP][:, i, 2 * P * h : 2 * P * (h + 1)].bitcast(FP4X4),
+                lhsT_scale=w_sc[:, e * PASSES + a, P * h : P * (h + 1)],
+                rhs=words[a, e // GROUP][:, (e % GROUP) * C : (e % GROUP + 1) * C].bitcast(FP8X4),
+                rhs_scale=(slot_bytes1 if a else slot_bytes)[:, e * C : (e + 1) * C],
+                start=(a == 0),
+                stop=(a == PASSES - 1),
+            )
+
+        def experts(lo, hi, halves=range(HALVES), step=1, held=None):
             for h in halves:
                 bank = next_bank() if held is None else held
                 for e in range(lo // C, hi // C)[::step]:
-                    cols = slice(e * C, (e + 1) * C)
                     for a in range(PASSES):
-                        i = (e % GROUP) * PASSES + a
-                        nc.tensor.matmul_mx(
-                            out=bank[:, e * C - lo : (e + 1) * C - lo],
-                            lhsT=w_t[e // GROUP][:, i, 2 * P * h : 2 * P * (h + 1)].bitcast(FP4X4),
-                            lhsT_scale=w_sc[:, e * PASSES + a, P * h : P * (h + 1)],
-                            rhs=words[a, e // GROUP][:, (e % GROUP) * C : (e % GROUP + 1) * C].bitcast(FP8X4),
-                            rhs_scale=(slot_bytes1 if a else slot_bytes)[:, cols],
-                            start=(a == 0),
-                            stop=(a == PASSES - 1),
-                        )
+                        one_pass(e, h, a, bank[:, e * C - lo : (e + 1) * C - lo])
                 nc.scalar.copy(y[h][:, lo:hi], bank[:, 0 : hi - lo])
 
         def gather_group(kind, g):
@@ -150,7 +152,7 @@ def tile_moe_tk_lin_none_kernel(
         def shift(lo, hi):
             nc.gpsimd.dma_start(slot_bytes1[0:112, lo:hi].bitcast(I32), slot_bytes[4:116, lo:hi].bitcast(I32))
 
-        for (lo, hi), cut in zip(LOADS[0], (128, 512, 736)):
+        for (lo, hi), cut in zip(LOADS[0], (128, 464, 688)):
             cast(nc.scalar.copy, 0, lo, lo, cut)
             cast(nc.vector.tensor_copy, 0, lo, cut, hi)
             if lo == 0:
@@ -175,13 +177,16 @@ def tile_moe_tk_lin_none_kernel(
         gather_group(1, 4)
         experts(4 * CHUNK, 5 * CHUNK, (0,))
         gather_group(0, CHUNKS - 1)
-        lo = (CHUNKS - 1) * CHUNK
-        for width in (256, 128, 128):
-            gather_words(1, lo, lo + width)
-            experts(lo, lo + width, (0,))
-            lo += width
-        experts(5 * CHUNK, 6 * CHUNK, (1,), banks[0], -1)
-        experts(4 * CHUNK, 5 * CHUNK, (1,), banks[5])
+        own_bank = {e: next_bank() for e in range(E - GROUP, E)}
+        for e, bank in own_bank.items():
+            one_pass(e, 0, 0, bank[:, 0:C])
+        for first, count in ((E - 4, 2), (E - 2, 1), (E - 1, 1)):
+            gather_words(1, first * C, (first + count) * C)
+            for e in range(first, first + count):
+                one_pass(e, 0, 1, own_bank[e][:, 0:C])
+                nc.scalar.copy(y[0][:, e * C : (e + 1) * C], own_bank[e][:, 0:C])
+        experts((CHUNKS - 1) * CHUNK, SLOTS, (1,), -1)
+        experts(4 * CHUNK, 5 * CHUNK, (1,), held=own_bank[E - 1])
 
         def fetch(h, r, tile, lo, hi):
             nc.vector.tensor_tensor(

@@ -48,9 +48,6 @@ def tile_moe_tk_lin_none_kernel(
         tok_bytes = keep.tile([P, T], U8, name="tok_bytes", align_bytes=64)
         slot_bytes = keep.tile([P, SLOTS], U8, name="slot_bytes", align_bytes=64)
         slot_bytes1 = keep.tile([P, SLOTS], U8, name="slot_bytes1", align_bytes=64)
-        nc.gpsimd.memset(tok_bytes[:].bitcast(I32), 0)
-        nc.vector.memset(w_sc[:].rearrange("p a n -> p (a n)").bitcast(I32), 0)
-        nc.gpsimd.memset(slot_bytes1[:].bitcast(I32), 0)
         ident = keep.tile([P, P], F32, name="ident")
         make_identity(nc, ident[:])
 

@@ -26,7 +26,15 @@ W_BYTES = 2 * N
 GROUP = 4
 CHUNK = GROUP * C
 CHUNKS = SLOTS // CHUNK
-LOADS = (((0, 384), (384, 640), (640, 768)), ((0, 256), (256, 512), (512, 768)))
+RAISED = 4
+SCALE_ROWS = 100
+RING = 4
+LEAD = 2
+BANKS = 6
+
+LOADS = (((0, 256), (256, 512), (512, 640), (640, 768)), ((0, 256), (256, 512), (512, 768)))
+SCALAR_SHARE = (96, 96, 48, 48)
+BLOCKS = (((0, 512), (512, 768)), ((0, 256), (256, 512), (512, 768)))
 
 
 def tile_moe_tk_lin_none_kernel(
@@ -37,7 +45,7 @@ def tile_moe_tk_lin_none_kernel(
         lists = ctx.enter_context(tc.tile_pool(name="lists", bufs=1))
         keep = ctx.enter_context(tc.tile_pool(name="keep", bufs=1))
         stream = ctx.enter_context(tc.tile_pool(name="stream", bufs=CHUNKS))
-        ring = ctx.enter_context(tc.tile_pool(name="ring", bufs=4))
+        ring = ctx.enter_context(tc.tile_pool(name="ring", bufs=RING))
         psum = ctx.enter_context(tc.psum_pool(name="psum", bufs=1))
         turns = ctx.enter_context(tc.psum_pool(name="turns", bufs=2))
 
@@ -77,8 +85,8 @@ def tile_moe_tk_lin_none_kernel(
             tile = tile[:].rearrange("p (i c) -> p i c", c=W_BYTES)
             nc.sync.dma_start(tile.bitcast(I32), w_view[:, g * GROUP * PASSES : (g + 1) * GROUP * PASSES])
             w_t.append(tile)
-        for r, p in enumerate((pos1, pos2, pos3, pos4)):
-            nc.sync.dma_start(pos_t[r][:], p)
+        for r, pos in enumerate((pos1, pos2, pos3, pos4)):
+            nc.sync.dma_start(pos_t[r][:], pos)
         gate_t = [keep.tile([P, T], F32, name=f"gate{r}") for r in range(TOP)]
         for r in range(TOP):
             nc.sync.dma_start(gate_t[r][:], gate[r, 0:P])
@@ -97,7 +105,7 @@ def tile_moe_tk_lin_none_kernel(
         def quantise(a, lo, hi):
             nc.vector.quantize_mx(
                 out=codes[a][:, lo:hi].bitcast(FP8X4),
-                scales=tok_bytes[4 * a : P, lo:hi],
+                scales=tok_bytes[RAISED * a : P, lo:hi],
                 in_=grouped[a][:, lo:hi, :].rearrange("p w j -> p (w j)"),
             )
 
@@ -109,15 +117,23 @@ def tile_moe_tk_lin_none_kernel(
                 words[a, g][:, lo - g * CHUNK : hi - g * CHUNK], codes[a][:].indirect(offs_t[:, lo // 16 : hi // 16])
             )
 
-        def gather_bytes(lo, hi):
-            nc.vector.tensor_copy(slot_bytes[:, lo:hi], tok_bytes[:].indirect(offs_t[:, lo // 16 : hi // 16]))
+        def gather_chunk(a, g):
+            gather_words(a, g * CHUNK, (g + 1) * CHUNK)
 
-        banks = [psum.tile([P, CHUNK], F32, name=f"bank{i}") for i in range(6)]
-        turn_of = [0]
+        def gather_bytes(g):
+            lo, hi = g * CHUNK, (g + 1) * CHUNK
+            nc.vector.tensor_copy(slot_bytes[:, lo:hi], tok_bytes[:].indirect(offs_t[:, lo // 16 : hi // 16]))
+            nc.gpsimd.dma_start(
+                slot_bytes1[0:SCALE_ROWS, lo:hi].bitcast(I32),
+                slot_bytes[RAISED : RAISED + SCALE_ROWS, lo:hi].bitcast(I32),
+            )
+
+        banks = [psum.tile([P, CHUNK], F32, name=f"bank{i}") for i in range(BANKS)]
+        taken = []
 
         def next_bank():
-            turn_of[0] = turn_of[0] + 1
-            return banks[(turn_of[0] - 1) % 6]
+            taken.append(banks[len(taken) % BANKS])
+            return taken[-1]
 
         def one_pass(e, h, a, target):
             i = (e % GROUP) * PASSES + a
@@ -131,49 +147,35 @@ def tile_moe_tk_lin_none_kernel(
                 stop=(a == PASSES - 1),
             )
 
-        def experts(lo, hi, halves=range(HALVES), step=1, held=None):
-            for h in halves:
-                bank = next_bank() if held is None else held
-                for e in range(lo // C, hi // C)[::step]:
-                    for a in range(PASSES):
-                        one_pass(e, h, a, bank[:, e * C - lo : (e + 1) * C - lo])
-                nc.scalar.copy(y[h][:, lo:hi], bank[:, 0 : hi - lo])
+        def experts(g, h, bank, step=1):
+            for e in range(g * GROUP, (g + 1) * GROUP)[::step]:
+                for a in range(PASSES):
+                    one_pass(e, h, a, bank[:, (e % GROUP) * C : (e % GROUP + 1) * C])
+            nc.scalar.copy(y[h][:, g * CHUNK : (g + 1) * CHUNK], bank[:, 0:CHUNK])
 
-        def gather_group(kind, g):
-            lo, hi = g * CHUNK, (g + 1) * CHUNK
-            if kind == "b":
-                gather_bytes(lo, hi)
-            else:
-                gather_words(kind, lo, hi)
-
-        def shift(lo, hi):
-            nc.gpsimd.dma_start(slot_bytes1[0:112, lo:hi].bitcast(I32), slot_bytes[4:116, lo:hi].bitcast(I32))
-
-        for (lo, hi), cut in zip(LOADS[0], (128, 464, 688)):
-            cast(nc.scalar.copy, 0, lo, lo, cut)
-            cast(nc.vector.tensor_copy, 0, lo, cut, hi)
-            if lo == 0:
-                quantise(0, cut, hi)
-                quantise(0, lo, cut)
-            else:
-                quantise(0, lo, hi)
+        for (lo, hi), share in zip(LOADS[0], SCALAR_SHARE):
+            cast(nc.scalar.copy, 0, lo, lo, lo + share)
+            cast(nc.vector.tensor_copy, 0, lo, lo + share, hi)
+            quantise(0, lo, hi)
         for lo, hi in LOADS[1]:
             cast(nc.scalar.copy, 1, lo, lo, hi)
 
-        for g in range(4):
-            gather_group(0, g)
+        for g in range(RING):
+            gather_chunk(0, g)
         quantise(1, 0, 512)
-        quantise(1, 512, 768)
+        quantise(1, 512, T)
+
         for g in range(CHUNKS):
-            gather_group("b", g)
-            shift(g * CHUNK, (g + 1) * CHUNK)
-            if g >= 2:
-                gather_group(1, g - 2)
-                experts((g - 2) * CHUNK, (g - 1) * CHUNK)
-        gather_group(0, 4)
-        gather_group(1, 4)
-        experts(4 * CHUNK, 5 * CHUNK, (0,))
-        gather_group(0, CHUNKS - 1)
+            gather_bytes(g)
+            if g >= LEAD:
+                gather_chunk(1, g - LEAD)
+                for h in range(HALVES):
+                    experts(g - LEAD, h, next_bank())
+        second_last, last_chunk = CHUNKS - 2, CHUNKS - 1
+        gather_chunk(0, second_last)
+        gather_chunk(1, second_last)
+        experts(second_last, 0, next_bank())
+        gather_chunk(0, last_chunk)
         own_bank = {e: next_bank() for e in range(E - GROUP, E)}
         for e, bank in own_bank.items():
             one_pass(e, 0, 0, bank[:, 0:C])
@@ -182,16 +184,15 @@ def tile_moe_tk_lin_none_kernel(
             for e in range(first, first + count):
                 one_pass(e, 0, 1, own_bank[e][:, 0:C])
                 nc.scalar.copy(y[0][:, e * C : (e + 1) * C], own_bank[e][:, 0:C])
-        experts((CHUNKS - 1) * CHUNK, SLOTS, (1,), -1)
-        experts(4 * CHUNK, 5 * CHUNK, (1,), held=own_bank[E - 1])
+        experts(last_chunk, 1, next_bank(), -1)
+        experts(second_last, 1, own_bank[E - 1])
 
         def fetch(h, r, tile, lo, hi):
             nc.vector.tensor_tensor(
                 tile[:, lo:hi], y[h][:].indirect(pos_t[r][:, lo // 16 : hi // 16]), gate_t[r][:, lo:hi], MULT
             )
 
-        BLOCKS = (((0, 512), (512, 768)), ((0, 256), (256, 512), (512, 768)))
-        turned = {(1, b): banks[2 + b] for b in range(3)}
+        turned = {(1, b): banks[2 + b] for b in range(len(BLOCKS[1]))}
         prods = {}
 
         def product(h, r, lo=0, hi=T):
@@ -226,21 +227,22 @@ def tile_moe_tk_lin_none_kernel(
             for b in range(len(BLOCKS[h])):
                 turn(h, r, b)
 
-        for r in range(TOP - 1):
+        final = TOP - 1
+        for r in range(final):
             whole(0, r)
         backs = {(0, 1): turn_back(0, 1, banks[1])}
         whole(1, 0)
-        product(0, TOP - 1, 0, 512)
-        turn(0, TOP - 1, 0)
+        product(0, final, *BLOCKS[0][0])
+        turn(0, final, 0)
         back = turn_back(0, 0, banks[0])
-        total = keep.tile([P, 512], F32, name="total0_0")
-        nc.scalar.copy(total[:], back)
-        nc.sync.dma_start(out[0:P, 0:512], total[:])
+        early = keep.tile([P, BLOCKS[0][0][1]], F32, name="total0_0")
+        nc.scalar.copy(early[:], back)
+        nc.sync.dma_start(out[0:P, 0 : BLOCKS[0][0][1]], early[:])
         whole(1, 1)
         spare = turns.tile([P, CHUNK], F32, name="turned")
         for b, (lo, hi) in enumerate(BLOCKS[1]):
-            product(1, 2, lo, hi)
-            turn(1, 2, b)
+            product(1, final - 1, lo, hi)
+            turn(1, final - 1, b)
             backs[1, b] = turn_back(1, b, (banks[5], spare, banks[0])[b])
 
         last = keep.tile([P, T], F32, name="last")
@@ -251,11 +253,11 @@ def tile_moe_tk_lin_none_kernel(
             nc.vector.tensor_add(total[:], backs[h, b], prod[:, lo:hi])
             nc.sync.dma_start(out[h * P : (h + 1) * P, lo:hi], total[:])
 
-        product(0, TOP - 1, 512, 768)
-        fetch(1, TOP - 1, last, 0, 256)
-        finish(0, 1, prods[0, TOP - 1])
-        fetch(1, TOP - 1, last, 256, 512)
+        product(0, final, *BLOCKS[0][1])
+        fetch(1, final, last, *BLOCKS[1][0])
+        finish(0, 1, prods[0, final])
+        fetch(1, final, last, *BLOCKS[1][1])
         finish(1, 0, last)
-        fetch(1, TOP - 1, last, 512, 768)
+        fetch(1, final, last, *BLOCKS[1][2])
         finish(1, 1, last)
         finish(1, 2, last)

@@ -165,12 +165,19 @@ def tile_moe_tk_lin_none_kernel(
         quantise(1, 0, 512)
         quantise(1, 512, T)
 
-        for g in range(CHUNKS):
+        def both_halves(g):
+            gather_chunk(1, g)
+            for h in range(HALVES):
+                experts(g, h, next_bank())
+
+        for g in range(CHUNKS - 1):
             gather_bytes(g)
-            if g >= LEAD:
-                gather_chunk(1, g - LEAD)
-                for h in range(HALVES):
-                    experts(g - LEAD, h, next_bank())
+            if LEAD <= g < CHUNKS - 2:
+                both_halves(g - LEAD)
+        gather_bytes(CHUNKS - 1)
+        both_halves(CHUNKS - 4)
+        gather_chunk(1, CHUNKS - 3)
+        experts(CHUNKS - 3, 0, next_bank())
         second_last, last_chunk = CHUNKS - 2, CHUNKS - 1
         gather_chunk(0, second_last)
         gather_chunk(1, second_last)
@@ -186,6 +193,7 @@ def tile_moe_tk_lin_none_kernel(
                 nc.scalar.copy(y[0][:, e * C : (e + 1) * C], own_bank[e][:, 0:C])
         experts(last_chunk, 1, next_bank(), -1)
         experts(second_last, 1, own_bank[E - 1])
+        experts(CHUNKS - 3, 1, own_bank[E - 2])
 
         def fetch(h, r, tile, lo, hi):
             nc.vector.tensor_tensor(

@@ -22,6 +22,8 @@ FP8X4 = mybir.dt.float8_e4m3fn_x4
 FP4X4 = mybir.dt.float4_e2m1fn_x4
 MULT = mybir.AluOpType.mult
 
+COPY = mybir.ActivationFunctionType.Copy
+
 W_BYTES = 2 * N
 GROUP = 4
 CHUNK = GROUP * C
@@ -29,12 +31,13 @@ CHUNKS = SLOTS // CHUNK
 RAISED = 4
 SCALE_ROWS = 100
 RING = 4
-LEAD = 2
-BANKS = 6
+BANKS = 8
 
 LOADS = (((0, 256), (256, 512), (512, 640), (640, 768)), ((0, 256), (256, 512), (512, 768)))
 SCALAR_SHARE = (96, 96, 48, 48)
-BLOCKS = (((0, 512), (512, 768)), ((0, 256), (256, 512), (512, 768)))
+SPLIT = 384
+TURNED = (T - SPLIT) // P
+EARLY = TOP - 1
 
 
 def tile_moe_tk_lin_none_kernel(
@@ -47,7 +50,6 @@ def tile_moe_tk_lin_none_kernel(
         stream = ctx.enter_context(tc.tile_pool(name="stream", bufs=CHUNKS))
         ring = ctx.enter_context(tc.tile_pool(name="ring", bufs=RING))
         psum = ctx.enter_context(tc.psum_pool(name="psum", bufs=1))
-        turns = ctx.enter_context(tc.psum_pool(name="turns", bufs=2))
 
         offs_t = lists.tile([P, SLOTS // 16], U16, name="offs_t")
         pos_t = [lists.tile([P, T // 16], U16, name=f"pos{r}_t") for r in range(TOP)]
@@ -58,6 +60,9 @@ def tile_moe_tk_lin_none_kernel(
         slot_bytes1 = keep.tile([P, SLOTS], U8, name="slot_bytes1", align_bytes=64)
         ident = keep.tile([P, P], F32, name="ident")
         make_identity(nc, ident[:])
+        gate_rows = keep.tile([P, T - SPLIT], F32, name="gate_rows")
+        nc.gpsimd.memset(gate_rows[:], 0.0)
+        nc.gpsimd.dma_start(gate_rows[0:EARLY], gate[0:EARLY, 0, SPLIT:T])
 
         x_view = xT.rearrange("(a p j) t -> a p j t", a=PASSES, p=P, j=PACK)
         raw = {}
@@ -87,14 +92,18 @@ def tile_moe_tk_lin_none_kernel(
             w_t.append(tile)
         for r, pos in enumerate((pos1, pos2, pos3, pos4)):
             nc.sync.dma_start(pos_t[r][:], pos)
-        gate_t = [keep.tile([P, T], F32, name=f"gate{r}") for r in range(TOP)]
+        gate_t = [keep.tile([P, SPLIT if r < EARLY else T], F32, name=f"gate{r}") for r in range(TOP)]
         for r in range(TOP):
-            nc.sync.dma_start(gate_t[r][:], gate[r, 0:P])
+            nc.sync.dma_start(gate_t[r][:], gate[r, 0:P, 0 : SPLIT if r < EARLY else T])
 
         grouped = [keep.tile([P, T, PACK], BF16, name=f"grouped{a}", align_bytes=64) for a in range(PASSES)]
         codes = [keep.tile([P, T], U32, name=f"codes{a}", align_bytes=64) for a in range(PASSES)]
         words = {}
         y = [keep.tile([P, SLOTS], F32, name=f"y{h}") for h in range(HALVES)]
+        banks = [psum.tile([P, CHUNK], F32, name=f"bank{i}") for i in range(BANKS)]
+
+        def scalar_move(dst, src):
+            nc.scalar.activation(dst, src, COPY)
 
         def cast(engine_copy, a, load, lo, hi):
             engine_copy(
@@ -109,16 +118,16 @@ def tile_moe_tk_lin_none_kernel(
                 in_=grouped[a][:, lo:hi, :].rearrange("p w j -> p (w j)"),
             )
 
-        def gather_words(a, lo, hi):
+        def gather_words(a, lo, hi, tag=None):
             g = lo // CHUNK
             if lo == g * CHUNK:
-                words[a, g] = ring.tile([P, CHUNK], U32, name=f"words{a}", align_bytes=64)
+                words[a, g] = ring.tile([P, CHUNK], U32, name=f"words{a}", tag=tag or f"words{a}", align_bytes=64)
             nc.vector.tensor_copy(
                 words[a, g][:, lo - g * CHUNK : hi - g * CHUNK], codes[a][:].indirect(offs_t[:, lo // 16 : hi // 16])
             )
 
-        def gather_chunk(a, g):
-            gather_words(a, g * CHUNK, (g + 1) * CHUNK)
+        def gather_chunk(a, g, tag=None):
+            gather_words(a, g * CHUNK, (g + 1) * CHUNK, tag)
 
         def gather_bytes(g):
             lo, hi = g * CHUNK, (g + 1) * CHUNK
@@ -128,144 +137,166 @@ def tile_moe_tk_lin_none_kernel(
                 slot_bytes[RAISED : RAISED + SCALE_ROWS, lo:hi].bitcast(I32),
             )
 
-        banks = [psum.tile([P, CHUNK], F32, name=f"bank{i}") for i in range(BANKS)]
-        taken = []
+        def one_pass(a, first, count, pair):
+            for h in range(HALVES):
+                for e in range(first, first + count):
+                    i = (e % GROUP) * PASSES + a
+                    nc.tensor.matmul_mx(
+                        out=banks[2 * pair + h][:, (e - first) * C : (e - first + 1) * C],
+                        lhsT=w_t[e // GROUP][:, i, 2 * P * h : 2 * P * (h + 1)].bitcast(FP4X4),
+                        lhsT_scale=w_sc[:, e * PASSES + a, P * h : P * (h + 1)],
+                        rhs=words[a, e // GROUP][:, (e % GROUP) * C : (e % GROUP + 1) * C].bitcast(FP8X4),
+                        rhs_scale=(slot_bytes1 if a else slot_bytes)[:, e * C : (e + 1) * C],
+                        start=(a == 0 and e == first),
+                        stop=(a == PASSES - 1 and e == first + count - 1),
+                    )
 
-        def next_bank():
-            taken.append(banks[len(taken) % BANKS])
-            return taken[-1]
-
-        def one_pass(e, h, a, target):
-            i = (e % GROUP) * PASSES + a
-            nc.tensor.matmul_mx(
-                out=target,
-                lhsT=w_t[e // GROUP][:, i, 2 * P * h : 2 * P * (h + 1)].bitcast(FP4X4),
-                lhsT_scale=w_sc[:, e * PASSES + a, P * h : P * (h + 1)],
-                rhs=words[a, e // GROUP][:, (e % GROUP) * C : (e % GROUP + 1) * C].bitcast(FP8X4),
-                rhs_scale=(slot_bytes1 if a else slot_bytes)[:, e * C : (e + 1) * C],
-                start=(a == 0),
-                stop=(a == PASSES - 1),
-            )
-
-        def experts(g, h, bank, step=1):
-            for e in range(g * GROUP, (g + 1) * GROUP)[::step]:
-                for a in range(PASSES):
-                    one_pass(e, h, a, bank[:, (e % GROUP) * C : (e % GROUP + 1) * C])
-            nc.scalar.copy(y[h][:, g * CHUNK : (g + 1) * CHUNK], bank[:, 0:CHUNK])
+        def empty(engine_copy, h, first, count, pair):
+            engine_copy(y[h][:, first * C : (first + count) * C], banks[2 * pair + h][:, 0 : count * C])
 
         for (lo, hi), share in zip(LOADS[0], SCALAR_SHARE):
-            cast(nc.scalar.copy, 0, lo, lo, lo + share)
+            cast(scalar_move, 0, lo, lo, lo + share)
             cast(nc.vector.tensor_copy, 0, lo, lo + share, hi)
             quantise(0, lo, hi)
         for lo, hi in LOADS[1]:
-            cast(nc.scalar.copy, 1, lo, lo, hi)
+            cast(scalar_move, 1, lo, lo, hi)
+
+        for j in range(TURNED):
+            nc.tensor.transpose(banks[7][:, j * P : (j + 1) * P], gate_rows[:, j * P : (j + 1) * P], ident[:])
+        gate_cols = keep.tile([P, TURNED, EARLY], F32, name="gate_cols", tag=f"raw1_{LOADS[1][-1][0]}")
+        nc.scalar.copy(gate_cols[:], banks[7][:, 0 : TURNED * P].rearrange("p (j c) -> p j c", c=P)[:, :, 0:EARLY])
 
         for g in range(RING):
             gather_chunk(0, g)
         quantise(1, 0, 512)
         quantise(1, 512, T)
 
-        def both_halves(g):
+        def first_pass(g):
+            one_pass(0, g * GROUP, GROUP, g % 4)
+
+        def second_pass(g):
             gather_chunk(1, g)
+            one_pass(1, g * GROUP, GROUP, g % 4)
             for h in range(HALVES):
-                experts(g, h, next_bank())
+                empty(nc.scalar.copy, h, g * GROUP, GROUP, g % 4)
 
-        for g in range(CHUNKS - 1):
+        for g in range(3):
             gather_bytes(g)
-            if LEAD <= g < CHUNKS - 2:
-                both_halves(g - LEAD)
-        gather_bytes(CHUNKS - 1)
-        both_halves(CHUNKS - 4)
-        gather_chunk(1, CHUNKS - 3)
-        experts(CHUNKS - 3, 0, next_bank())
-        second_last, last_chunk = CHUNKS - 2, CHUNKS - 1
-        gather_chunk(0, second_last)
-        gather_chunk(1, second_last)
-        experts(second_last, 0, next_bank())
-        gather_chunk(0, last_chunk)
-        own_bank = {e: next_bank() for e in range(E - GROUP, E)}
-        for e, bank in own_bank.items():
-            one_pass(e, 0, 0, bank[:, 0:C])
-        for first, count in ((E - 4, 2), (E - 2, 1), (E - 1, 1)):
+            first_pass(g)
+        second_pass(0)
+        gather_bytes(3)
+        first_pass(3)
+        second_pass(1)
+        gather_bytes(4)
+        gather_bytes(5)
+        second_pass(2)
+        second_pass(3)
+        gather_chunk(0, 4)
+        first_pass(4)
+        second_pass(4)
+        gather_chunk(0, 5, "words1")
+        pieces = ((E - 4, 2, 1), (E - 2, 1, 2), (E - 1, 1, 3))
+        for first, count, pair in pieces:
+            one_pass(0, first, count, pair)
+        for first, count, pair in pieces:
             gather_words(1, first * C, (first + count) * C)
-            for e in range(first, first + count):
-                one_pass(e, 0, 1, own_bank[e][:, 0:C])
-                nc.scalar.copy(y[0][:, e * C : (e + 1) * C], own_bank[e][:, 0:C])
-        experts(last_chunk, 1, next_bank(), -1)
-        experts(second_last, 1, own_bank[E - 1])
-        experts(CHUNKS - 3, 1, own_bank[E - 2])
+            one_pass(1, first, count, pair)
+            empty(nc.scalar.copy, 0, first, count, pair)
+        for first, count, pair in pieces:
+            empty(nc.vector.tensor_copy, 1, first, count, pair)
 
-        def fetch(h, r, tile, lo, hi):
-            nc.vector.tensor_tensor(
-                tile[:, lo:hi], y[h][:].indirect(pos_t[r][:, lo // 16 : hi // 16]), gate_t[r][:, lo:hi], MULT
-            )
+        def window(h, r, lo, hi):
+            return y[h][:].indirect(pos_t[r][:, lo // 16 : hi // 16])
 
-        turned = {(1, b): banks[2 + b] for b in range(len(BLOCKS[1]))}
-        prods = {}
+        def turn(target, source, start, stop):
+            nc.tensor.matmul(target, lhsT=source, rhs=ident[:], is_transpose=True, start=start, stop=stop)
 
-        def product(h, r, lo=0, hi=T):
-            if lo == 0:
-                prods[h, r] = keep.tile([P, T], F32, name=f"prod{h}_{r}")
-            fetch(h, r, prods[h, r], lo, hi)
+        turned = banks[0:TURNED]
+        sums = banks[TURNED : TURNED + HALVES]
+        backs = banks[TURNED + HALVES :]
 
-        def turn(h, r, b):
-            lo, hi = BLOCKS[h][b]
-            if (h, b) not in turned:
-                turned[h, b] = turns.tile([P, CHUNK], F32, name="turned")
-            for c in range(lo, hi, P):
-                nc.tensor.matmul(
-                    turned[h, b][:, c - lo : c - lo + P],
-                    lhsT=prods[h, r][:, c : c + P],
-                    rhs=ident[:],
-                    is_transpose=True,
-                    start=(r == 0 and c == lo),
-                    stop=(r == (TOP - 1 if (h, b) == (0, 0) else TOP - 2) and c == hi - P),
+        def product(h, r):
+            tile = keep.tile([P, SPLIT], F32, name=f"prod{h}_{r}")
+            nc.vector.tensor_tensor(tile[:], window(h, r, 0, SPLIT), gate_t[r][:, 0:SPLIT], MULT)
+            for c in range(0, SPLIT, P):
+                turn(sums[h][:, c : c + P], tile[:, c : c + P], r == 0 and c == 0, r == TOP - 1 and c == SPLIT - P)
+
+        fetched = {}
+
+        def fetch(h, r):
+            fetched[h, r] = keep.tile([P, T - SPLIT], F32, name=f"fetched{h}_{r}")
+            scalar_move(fetched[h, r][:], window(h, r, SPLIT, T))
+
+        def turn_fetched(r, j):
+            for h in range(HALVES):
+                at = (r % 2) * N + h * P
+                turn(turned[j][:, at : at + P], fetched[h, r][:, j * P : (j + 1) * P], True, True)
+
+        scaled = {}
+
+        def scale(r, j):
+            scaled[r, j] = keep.tile([P, N], F32, name=f"scaled{r}_{j}")
+            at = (r % 2) * N
+            nc.scalar.activation(scaled[r, j][:], turned[j][:, at : at + N], COPY, scale=gate_cols[:, j, r : r + 1])
+
+        def add_back(r, j):
+            for h in range(HALVES):
+                turn(
+                    backs[j][:, h * P : (h + 1) * P],
+                    scaled[r, j][:, h * P : (h + 1) * P],
+                    r == 0 and h == 0,
+                    r == EARLY - 1 and h == HALVES - 1,
                 )
 
-        def turn_back(h, b, bank):
-            lo, hi = BLOCKS[h][b]
-            staged = keep.tile([P, hi - lo], F32, name=f"staged{h}_{b}")
-            nc.scalar.copy(staged[:], turned[h, b][:, 0 : hi - lo])
-            for c in range(0, hi - lo, P):
-                nc.tensor.transpose(bank[:, c : c + P], staged[:, c : c + P], ident[:])
-            return bank[:, 0 : hi - lo]
+        def turn_back(h):
+            staged = keep.tile([P, SPLIT], F32, name=f"staged{h}")
+            nc.scalar.copy(staged[:], sums[h][:, 0:SPLIT])
+            for c in range(0, SPLIT, P):
+                turn(sums[h][:, c : c + P], staged[:, c : c + P], True, True)
 
-        def whole(h, r):
-            product(h, r)
-            for b in range(len(BLOCKS[h])):
-                turn(h, r, b)
+        def store_low(h):
+            total = keep.tile([P, SPLIT], F32, name=f"total{h}")
+            nc.scalar.copy(total[:], sums[h][:, 0:SPLIT])
+            nc.sync.dma_start(out[h * P : (h + 1) * P, 0:SPLIT], total[:])
 
-        final = TOP - 1
-        for r in range(final):
-            whole(0, r)
-        backs = {(0, 1): turn_back(0, 1, banks[1])}
-        whole(1, 0)
-        product(0, final, *BLOCKS[0][0])
-        turn(0, final, 0)
-        back = turn_back(0, 0, banks[0])
-        early = keep.tile([P, BLOCKS[0][0][1]], F32, name="total0_0")
-        nc.scalar.copy(early[:], back)
-        nc.sync.dma_start(out[0:P, 0 : BLOCKS[0][0][1]], early[:])
-        whole(1, 1)
-        spare = turns.tile([P, CHUNK], F32, name="turned")
-        for b, (lo, hi) in enumerate(BLOCKS[1]):
-            product(1, final - 1, lo, hi)
-            turn(1, final - 1, b)
-            backs[1, b] = turn_back(1, b, (banks[5], spare, banks[0])[b])
-
-        last = keep.tile([P, T], F32, name="last")
-
-        def finish(h, b, prod):
-            lo, hi = BLOCKS[h][b]
-            total = keep.tile([P, hi - lo], F32, name=f"total{h}_{b}")
-            nc.vector.tensor_add(total[:], backs[h, b], prod[:, lo:hi])
-            nc.sync.dma_start(out[h * P : (h + 1) * P, lo:hi], total[:])
-
-        product(0, final, *BLOCKS[0][1])
-        fetch(1, final, last, *BLOCKS[1][0])
-        finish(0, 1, prods[0, final])
-        fetch(1, final, last, *BLOCKS[1][1])
-        finish(1, 0, last)
-        fetch(1, final, last, *BLOCKS[1][2])
-        finish(1, 1, last)
-        finish(1, 2, last)
+        fetch(0, 0)
+        product(0, 0)
+        fetch(1, 0)
+        product(0, 1)
+        for j in range(TURNED):
+            turn_fetched(0, j)
+        fetch(0, 1)
+        product(0, 2)
+        fetch(1, 1)
+        product(0, 3)
+        for j in range(TURNED):
+            turn_fetched(1, j)
+        fetch(0, 2)
+        product(1, 0)
+        fetch(1, 2)
+        product(1, 1)
+        for j in range(TURNED):
+            scale(0, j)
+            scale(1, j)
+            turn_fetched(2, j)
+            add_back(0, j)
+            add_back(1, j)
+            if j < 2:
+                product(1, 2 + j)
+        turn_back(0)
+        last = keep.tile([P, HALVES, T - SPLIT], F32, name="last")
+        for h in range(HALVES):
+            nc.vector.tensor_tensor(last[:, h, :], window(h, EARLY, SPLIT, T), gate_t[EARLY][:, SPLIT:T], MULT)
+        for j in range(TURNED):
+            scale(2, j)
+            add_back(2, j)
+        turn_back(1)
+        store_low(0)
+        out_view = out.rearrange("(h p) t -> p h t", p=P)
+        for j in range(TURNED):
+            total = keep.tile([P, HALVES, P], F32, name=f"high{j}")
+            nc.vector.tensor_add(
+                total[:], backs[j][:, 0:N].rearrange("p (h c) -> p h c", c=P), last[:, :, j * P : (j + 1) * P]
+            )
+            nc.sync.dma_start(out_view[:, :, SPLIT + j * P : SPLIT + (j + 1) * P], total[:])
+        store_low(1)

@@ -49,6 +49,7 @@ def tile_moe_tk_lin_none_kernel(
         keep = ctx.enter_context(tc.tile_pool(name="keep", bufs=1))
         stream = ctx.enter_context(tc.tile_pool(name="stream", bufs=CHUNKS))
         ring = ctx.enter_context(tc.tile_pool(name="ring", bufs=RING))
+        held = ctx.enter_context(tc.tile_pool(name="held", bufs=3))
         psum = ctx.enter_context(tc.psum_pool(name="psum", bufs=1))
 
         offs_t = lists.tile([P, SLOTS // 16], U16, name="offs_t")
@@ -215,29 +216,32 @@ def tile_moe_tk_lin_none_kernel(
         sums = banks[TURNED : TURNED + HALVES]
         backs = banks[TURNED + HALVES :]
 
+        prods = {}
+
         def product(h, r):
-            tile = keep.tile([P, SPLIT], F32, name=f"prod{h}_{r}")
-            nc.vector.tensor_tensor(tile[:], window(h, r, 0, SPLIT), gate_t[r][:, 0:SPLIT], MULT)
+            prods[h, r] = keep.tile([P, SPLIT], F32, name=f"prod{h}_{r}")
+            nc.vector.tensor_tensor(prods[h, r][:], window(h, r, 0, SPLIT), gate_t[r][:, 0:SPLIT], MULT)
+
+        def turn_product(h, r):
             for c in range(0, SPLIT, P):
-                turn(sums[h][:, c : c + P], tile[:, c : c + P], r == 0 and c == 0, r == TOP - 1 and c == SPLIT - P)
+                first, final = r == 0 and c == 0, r == EARLY - 1 and c == SPLIT - P
+                turn(sums[h][:, c : c + P], prods[h, r][:, c : c + P], first, final)
 
         fetched = {}
 
         def fetch(h, r):
-            fetched[h, r] = keep.tile([P, T - SPLIT], F32, name=f"fetched{h}_{r}")
+            fetched[h, r] = held.tile([P, T - SPLIT], F32, name="fetched")
             scalar_move(fetched[h, r][:], window(h, r, SPLIT, T))
 
-        def turn_fetched(r, j):
-            for h in range(HALVES):
-                at = (r % 2) * N + h * P
-                turn(turned[j][:, at : at + P], fetched[h, r][:, j * P : (j + 1) * P], True, True)
+        def turn_fetched(h, r):
+            for j in range(TURNED):
+                turn(turned[j][:, h * P : (h + 1) * P], fetched[h, r][:, j * P : (j + 1) * P], True, True)
 
         scaled = {}
 
         def scale(r, j):
             scaled[r, j] = keep.tile([P, N], F32, name=f"scaled{r}_{j}")
-            at = (r % 2) * N
-            nc.scalar.activation(scaled[r, j][:], turned[j][:, at : at + N], COPY, scale=gate_cols[:, j, r : r + 1])
+            nc.scalar.activation(scaled[r, j][:], turned[j][:, 0:N], COPY, scale=gate_cols[:, j, r : r + 1])
 
         def add_back(r, j):
             for h in range(HALVES):
@@ -254,49 +258,59 @@ def tile_moe_tk_lin_none_kernel(
             for c in range(0, SPLIT, P):
                 turn(sums[h][:, c : c + P], staged[:, c : c + P], True, True)
 
-        def store_low(h):
-            total = keep.tile([P, SPLIT], F32, name=f"total{h}")
-            nc.scalar.copy(total[:], sums[h][:, 0:SPLIT])
+        def turn_one(h, r, j):
+            turn(turned[j][:, h * P : (h + 1) * P], fetched[h, r][:, j * P : (j + 1) * P], True, True)
+
+        def scale_all(r):
+            for j in range(TURNED):
+                scale(r, j)
+                if r + 1 < EARLY:
+                    turn_one(0, r + 1, j)
+                add_back(r, j)
+
+        last = keep.tile([P, HALVES, T], F32, name="last")
+
+        def finish_low(h):
+            total = keep.tile([P, SPLIT], F32, name=f"low{h}")
+            nc.vector.tensor_add(total[:], sums[h][:, 0:SPLIT], last[:, h, 0:SPLIT])
             nc.sync.dma_start(out[h * P : (h + 1) * P, 0:SPLIT], total[:])
 
-        fetch(0, 0)
-        product(0, 0)
-        fetch(1, 0)
-        product(0, 1)
-        for j in range(TURNED):
-            turn_fetched(0, j)
-        fetch(0, 1)
-        product(0, 2)
-        fetch(1, 1)
-        product(0, 3)
-        for j in range(TURNED):
-            turn_fetched(1, j)
-        fetch(0, 2)
-        product(1, 0)
-        fetch(1, 2)
-        product(1, 1)
-        for j in range(TURNED):
-            scale(0, j)
-            scale(1, j)
-            turn_fetched(2, j)
-            add_back(0, j)
-            add_back(1, j)
-            if j < 2:
-                product(1, 2 + j)
-        turn_back(0)
-        last = keep.tile([P, HALVES, T - SPLIT], F32, name="last")
+        def fourth(h):
+            nc.vector.tensor_tensor(last[:, h, :], window(h, EARLY, 0, T), gate_t[EARLY][:], MULT)
+
         for h in range(HALVES):
-            nc.vector.tensor_tensor(last[:, h, :], window(h, EARLY, SPLIT, T), gate_t[EARLY][:, SPLIT:T], MULT)
-        for j in range(TURNED):
-            scale(2, j)
-            add_back(2, j)
+            for r in range(EARLY):
+                product(h, r)
+        fetch(0, 0)
+        turn_fetched(0, 0)
+        turn_product(0, 0)
+        fetch(1, 0)
+        turn_fetched(1, 0)
+        fetch(0, 1)
+        turn_product(0, 1)
+        turn_product(0, 2)
+        scale_all(0)
+        fetch(1, 1)
+        turn_fetched(1, 1)
+        fetch(0, 2)
+        turn_product(1, 0)
+        turn_back(0)
+        turn_product(1, 1)
+        fourth(0)
+        scale_all(1)
+        turn_product(1, 2)
+        fetch(1, 2)
+        turn_fetched(1, 2)
+        finish_low(0)
+        fourth(1)
         turn_back(1)
-        store_low(0)
+        scale_all(2)
+        finish_low(1)
         out_view = out.rearrange("(h p) t -> p h t", p=P)
         for j in range(TURNED):
             total = keep.tile([P, HALVES, P], F32, name=f"high{j}")
+            lo = SPLIT + j * P
             nc.vector.tensor_add(
-                total[:], backs[j][:, 0:N].rearrange("p (h c) -> p h c", c=P), last[:, :, j * P : (j + 1) * P]
+                total[:], backs[j][:, 0:N].rearrange("p (h c) -> p h c", c=P), last[:, :, lo : lo + P]
             )
-            nc.sync.dma_start(out_view[:, :, SPLIT + j * P : SPLIT + (j + 1) * P], total[:])
-        store_low(1)
+            nc.sync.dma_start(out_view[:, :, lo : lo + P], total[:])

@@ -49,7 +49,7 @@ def tile_moe_tk_lin_none_kernel(
         keep = ctx.enter_context(tc.tile_pool(name="keep", bufs=1))
         stream = ctx.enter_context(tc.tile_pool(name="stream", bufs=CHUNKS))
         ring = ctx.enter_context(tc.tile_pool(name="ring", bufs=RING))
-        held = ctx.enter_context(tc.tile_pool(name="held", bufs=3))
+        held = ctx.enter_context(tc.tile_pool(name="held", bufs=4))
         psum = ctx.enter_context(tc.psum_pool(name="psum", bufs=1))
 
         offs_t = lists.tile([P, SLOTS // 16], U16, name="offs_t")
@@ -261,11 +261,11 @@ def tile_moe_tk_lin_none_kernel(
         def turn_one(h, r, j):
             turn(turned[j][:, h * P : (h + 1) * P], fetched[h, r][:, j * P : (j + 1) * P], True, True)
 
-        def scale_all(r):
+        def scale_all(r, halves):
             for j in range(TURNED):
                 scale(r, j)
-                if r + 1 < EARLY:
-                    turn_one(0, r + 1, j)
+                for h in halves:
+                    turn_one(h, r + 1, j)
                 add_back(r, j)
 
         last = keep.tile([P, HALVES, T], F32, name="last")
@@ -275,37 +275,34 @@ def tile_moe_tk_lin_none_kernel(
             nc.vector.tensor_add(total[:], sums[h][:, 0:SPLIT], last[:, h, 0:SPLIT])
             nc.sync.dma_start(out[h * P : (h + 1) * P, 0:SPLIT], total[:])
 
-        def fourth(h):
-            nc.vector.tensor_tensor(last[:, h, :], window(h, EARLY, 0, T), gate_t[EARLY][:], MULT)
+        def fourth(h, lo, hi):
+            nc.vector.tensor_tensor(last[:, h, lo:hi], window(h, EARLY, lo, hi), gate_t[EARLY][:, lo:hi], MULT)
 
         for h in range(HALVES):
             for r in range(EARLY):
                 product(h, r)
-        fetch(0, 0)
-        turn_fetched(0, 0)
-        turn_product(0, 0)
-        fetch(1, 0)
-        turn_fetched(1, 0)
-        fetch(0, 1)
-        turn_product(0, 1)
+        for h in range(HALVES):
+            fetch(h, 0)
+            turn_fetched(h, 0)
+            turn_product(0, h)
+        for h in range(HALVES):
+            fetch(h, 1)
         turn_product(0, 2)
-        scale_all(0)
-        fetch(1, 1)
-        turn_fetched(1, 1)
+        scale_all(0, (0, 1))
         fetch(0, 2)
         turn_product(1, 0)
         turn_back(0)
         turn_product(1, 1)
-        fourth(0)
-        scale_all(1)
         turn_product(1, 2)
         fetch(1, 2)
-        turn_fetched(1, 2)
-        finish_low(0)
-        fourth(1)
         turn_back(1)
-        scale_all(2)
+        fourth(0, 0, T)
+        scale_all(1, (0, 1))
+        fourth(1, 0, SPLIT)
+        finish_low(0)
+        fourth(1, SPLIT, T)
         finish_low(1)
+        scale_all(2, ())
         out_view = out.rearrange("(h p) t -> p h t", p=P)
         for j in range(TURNED):
             total = keep.tile([P, HALVES, P], F32, name=f"high{j}")

@@ -261,9 +261,23 @@ def tile_moe_tk_lin_none_kernel(
         def turn_one(h, r, j):
             turn(turned[j][:, h * P : (h + 1) * P], fetched[h, r][:, j * P : (j + 1) * P], True, True)
 
+        def warm_up(bank):
+            for a in range(PASSES):
+                nc.tensor.matmul_mx(
+                    out=bank[:],
+                    lhsT=w_t[CHUNKS - 1][:, a, 0 : 2 * P].bitcast(FP4X4),
+                    lhsT_scale=w_sc[:, (E - GROUP) * PASSES + a, 0:P],
+                    rhs=words[a, CHUNKS - 1][:].bitcast(FP8X4),
+                    rhs_scale=(slot_bytes1 if a else slot_bytes)[:, SLOTS - CHUNK : SLOTS],
+                    start=True,
+                    stop=True,
+                )
+
         def scale_all(r, halves):
             for j in range(TURNED):
                 scale(r, j)
+                if (r, j) == (0, 0):
+                    warm_up(turned[j])
                 for h in halves:
                     turn_one(h, r + 1, j)
                 add_back(r, j)

@@ -204,7 +204,7 @@ def tile_moe_tk_lin_none_kernel(
             one_pass(1, first, count, pair)
             empty(nc.scalar.copy, 0, first, count, pair)
         for first, count, pair in pieces:
-            empty(nc.vector.tensor_copy, 1, first, count, pair)
+            empty(nc.scalar.copy if first == E - 1 else nc.vector.tensor_copy, 1, first, count, pair)
 
         def window(h, r, lo, hi):
             return y[h][:].indirect(pos_t[r][:, lo // 16 : hi // 16])
@@ -252,11 +252,15 @@ def tile_moe_tk_lin_none_kernel(
                     r == EARLY - 1 and h == HALVES - 1,
                 )
 
+        staged = {}
+
+        def stage(h):
+            staged[h] = keep.tile([P, SPLIT], F32, name=f"staged{h}")
+            nc.scalar.copy(staged[h][:], sums[h][:, 0:SPLIT])
+
         def turn_back(h):
-            staged = keep.tile([P, SPLIT], F32, name=f"staged{h}")
-            nc.scalar.copy(staged[:], sums[h][:, 0:SPLIT])
             for c in range(0, SPLIT, P):
-                turn(sums[h][:, c : c + P], staged[:, c : c + P], True, True)
+                turn(sums[h][:, c : c + P], staged[h][:, c : c + P], True, True)
 
         def turn_one(h, r, j):
             turn(turned[j][:, h * P : (h + 1) * P], fetched[h, r][:, j * P : (j + 1) * P], True, True)
@@ -272,15 +276,6 @@ def tile_moe_tk_lin_none_kernel(
                     start=True,
                     stop=True,
                 )
-
-        def scale_all(r, halves):
-            for j in range(TURNED):
-                scale(r, j)
-                if (r, j) == (0, 0):
-                    warm_up(turned[j])
-                for h in halves:
-                    turn_one(h, r + 1, j)
-                add_back(r, j)
 
         last = keep.tile([P, HALVES, T], F32, name="last")
 
@@ -302,21 +297,34 @@ def tile_moe_tk_lin_none_kernel(
         for h in range(HALVES):
             fetch(h, 1)
         turn_product(0, 2)
-        scale_all(0, (0, 1))
-        fetch(0, 2)
         turn_product(1, 0)
-        turn_back(0)
         turn_product(1, 1)
+        for j in range(TURNED):
+            scale(0, j)
+            if j == 0:
+                warm_up(turned[j])
+            for h in range(HALVES):
+                turn_one(h, 1, j)
+        fetch(0, 2)
         turn_product(1, 2)
+        stage(0)
+        turn_back(0)
         fetch(1, 2)
-        turn_back(1)
         fourth(0, 0, T)
-        scale_all(1, (0, 1))
-        fourth(1, 0, SPLIT)
-        finish_low(0)
-        fourth(1, SPLIT, T)
-        finish_low(1)
-        scale_all(2, ())
+        fourth(1, 0, T)
+        for j in range(TURNED):
+            scale(1, j)
+            for h in range(HALVES):
+                turn_one(h, 2, j)
+            add_back(0, j)
+            add_back(1, j)
+        stage(1)
+        turn_back(1)
+        for h in range(HALVES):
+            finish_low(h)
+        for j in range(TURNED):
+            scale(2, j)
+            add_back(2, j)
         out_view = out.rearrange("(h p) t -> p h t", p=P)
         for j in range(TURNED):
             total = keep.tile([P, HALVES, P], F32, name=f"high{j}")

@@ -49,7 +49,6 @@ def tile_moe_tk_lin_none_kernel(
         keep = ctx.enter_context(tc.tile_pool(name="keep", bufs=1))
         stream = ctx.enter_context(tc.tile_pool(name="stream", bufs=CHUNKS))
         ring = ctx.enter_context(tc.tile_pool(name="ring", bufs=RING))
-        held = ctx.enter_context(tc.tile_pool(name="held", bufs=4))
         psum = ctx.enter_context(tc.psum_pool(name="psum", bufs=1))
 
         offs_t = lists.tile([P, SLOTS // 16], U16, name="offs_t")
@@ -219,7 +218,7 @@ def tile_moe_tk_lin_none_kernel(
         prods = {}
 
         def product(h, r):
-            prods[h, r] = keep.tile([P, SPLIT], F32, name=f"prod{h}_{r}")
+            prods[h, r] = keep.tile([P, SPLIT], F32, name=f"prod{h}_{r}", tag=f"prod{h}_{r}")
             nc.vector.tensor_tensor(prods[h, r][:], window(h, r, 0, SPLIT), gate_t[r][:, 0:SPLIT], MULT)
 
         def turn_product(h, r):
@@ -229,19 +228,20 @@ def tile_moe_tk_lin_none_kernel(
 
         fetched = {}
 
-        def fetch(h, r):
-            fetched[h, r] = held.tile([P, T - SPLIT], F32, name="fetched")
+        def fetch(h, r, tag=None):
+            fetched[h, r] = keep.tile([P, T - SPLIT], F32, name=f"fetched{h}_{r}", tag=tag or f"fetched{h}_{r}")
             scalar_move(fetched[h, r][:], window(h, r, SPLIT, T))
 
         def turn_fetched(h, r):
             for j in range(TURNED):
-                turn(turned[j][:, h * P : (h + 1) * P], fetched[h, r][:, j * P : (j + 1) * P], True, True)
+                turn_one(h, r, j)
 
         scaled = {}
 
         def scale(r, j):
             scaled[r, j] = keep.tile([P, N], F32, name=f"scaled{r}_{j}")
-            nc.scalar.activation(scaled[r, j][:], turned[j][:, 0:N], COPY, scale=gate_cols[:, j, r : r + 1])
+            at = (r % 2) * N
+            nc.scalar.activation(scaled[r, j][:], turned[j][:, at : at + N], COPY, scale=gate_cols[:, j, r : r + 1])
 
         def add_back(r, j):
             for h in range(HALVES):
@@ -263,16 +263,17 @@ def tile_moe_tk_lin_none_kernel(
                 turn(sums[h][:, c : c + P], staged[h][:, c : c + P], True, True)
 
         def turn_one(h, r, j):
-            turn(turned[j][:, h * P : (h + 1) * P], fetched[h, r][:, j * P : (j + 1) * P], True, True)
+            at = (r % 2) * N + h * P
+            turn(turned[j][:, at : at + P], fetched[h, r][:, j * P : (j + 1) * P], True, True)
 
         def warm_up(bank):
-            for a in range(PASSES):
+            for a, lo in ((0, 0), (0, N), (1, 0), (1, N)):
                 nc.tensor.matmul_mx(
-                    out=bank[:],
+                    out=bank[:, 0:N],
                     lhsT=w_t[CHUNKS - 1][:, a, 0 : 2 * P].bitcast(FP4X4),
                     lhsT_scale=w_sc[:, (E - GROUP) * PASSES + a, 0:P],
-                    rhs=words[a, CHUNKS - 1][:].bitcast(FP8X4),
-                    rhs_scale=(slot_bytes1 if a else slot_bytes)[:, SLOTS - CHUNK : SLOTS],
+                    rhs=words[a, CHUNKS - 1][:, lo : lo + N].bitcast(FP8X4),
+                    rhs_scale=(slot_bytes1 if a else slot_bytes)[:, SLOTS - CHUNK + lo : SLOTS - CHUNK + lo + N],
                     start=True,
                     stop=True,
                 )
@@ -296,27 +297,28 @@ def tile_moe_tk_lin_none_kernel(
             turn_product(0, h)
         for h in range(HALVES):
             fetch(h, 1)
+        turn_fetched(0, 1)
         turn_product(0, 2)
         turn_product(1, 0)
-        turn_product(1, 1)
         for j in range(TURNED):
             scale(0, j)
             if j == 0:
                 warm_up(turned[j])
-            for h in range(HALVES):
-                turn_one(h, 1, j)
-        fetch(0, 2)
+            turn_one(1, 1, j)
+        fetch(0, 2, "fetched0_1")
+        turn_product(1, 1)
         turn_product(1, 2)
         stage(0)
+        for j in range(TURNED):
+            add_back(0, j)
         turn_back(0)
-        fetch(1, 2)
+        fetch(1, 2, "prod0_2")
         fourth(0, 0, T)
         fourth(1, 0, T)
         for j in range(TURNED):
             scale(1, j)
             for h in range(HALVES):
                 turn_one(h, 2, j)
-            add_back(0, j)
             add_back(1, j)
         stage(1)
         turn_back(1)

@@ -240,8 +240,7 @@ def tile_moe_tk_lin_none_kernel(
 
         def scale(r, j):
             scaled[r, j] = keep.tile([P, N], F32, name=f"scaled{r}_{j}")
-            at = (r % 2) * N
-            nc.scalar.activation(scaled[r, j][:], turned[j][:, at : at + N], COPY, scale=gate_cols[:, j, r : r + 1])
+            nc.scalar.activation(scaled[r, j][:], turned[j][:, 0:N], COPY, scale=gate_cols[:, j, r : r + 1])
 
         def add_back(r, j):
             for h in range(HALVES):
@@ -255,7 +254,7 @@ def tile_moe_tk_lin_none_kernel(
         staged = {}
 
         def stage(h):
-            staged[h] = keep.tile([P, SPLIT], F32, name=f"staged{h}")
+            staged[h] = keep.tile([P, SPLIT], F32, name=f"staged{h}", tag=f"staged{h}")
             nc.scalar.copy(staged[h][:], sums[h][:, 0:SPLIT])
 
         def turn_back(h):
@@ -263,31 +262,37 @@ def tile_moe_tk_lin_none_kernel(
                 turn(sums[h][:, c : c + P], staged[h][:, c : c + P], True, True)
 
         def turn_one(h, r, j):
-            at = (r % 2) * N + h * P
-            turn(turned[j][:, at : at + P], fetched[h, r][:, j * P : (j + 1) * P], True, True)
+            turn(turned[j][:, h * P : (h + 1) * P], fetched[h, r][:, j * P : (j + 1) * P], True, True)
 
         def warm_up(bank):
-            for a, lo in ((0, 0), (0, N), (1, 0), (1, N)):
+            for a in range(PASSES):
                 nc.tensor.matmul_mx(
-                    out=bank[:, 0:N],
+                    out=bank[:],
                     lhsT=w_t[CHUNKS - 1][:, a, 0 : 2 * P].bitcast(FP4X4),
                     lhsT_scale=w_sc[:, (E - GROUP) * PASSES + a, 0:P],
-                    rhs=words[a, CHUNKS - 1][:, lo : lo + N].bitcast(FP8X4),
-                    rhs_scale=(slot_bytes1 if a else slot_bytes)[:, SLOTS - CHUNK + lo : SLOTS - CHUNK + lo + N],
+                    rhs=words[a, CHUNKS - 1][:].bitcast(FP8X4),
+                    rhs_scale=(slot_bytes1 if a else slot_bytes)[:, SLOTS - CHUNK : SLOTS],
                     start=True,
                     stop=True,
                 )
 
-        last = keep.tile([P, HALVES, T], F32, name="last")
-
         def finish_low(h):
             total = keep.tile([P, SPLIT], F32, name=f"low{h}")
-            nc.vector.tensor_add(total[:], sums[h][:, 0:SPLIT], last[:, h, 0:SPLIT])
+            nc.vector.tensor_add(total[:], sums[h][:, 0:SPLIT], last_low[:, h, :])
             nc.sync.dma_start(out[h * P : (h + 1) * P, 0:SPLIT], total[:])
 
-        def fourth(h, lo, hi):
-            nc.vector.tensor_tensor(last[:, h, lo:hi], window(h, EARLY, lo, hi), gate_t[EARLY][:, lo:hi], MULT)
+        def fourth(tile, lo, hi):
+            for h in range(HALVES):
+                nc.vector.tensor_tensor(tile[:, h, :], window(h, EARLY, lo, hi), gate_t[EARLY][:, lo:hi], MULT)
 
+        def scale_all(r):
+            for j in range(TURNED):
+                scale(r, j)
+                if r + 1 < EARLY:
+                    turn_one(0, r + 1, j)
+                add_back(r, j)
+
+        warm_up(backs[-1])
         for h in range(HALVES):
             for r in range(EARLY):
                 product(h, r)
@@ -295,43 +300,33 @@ def tile_moe_tk_lin_none_kernel(
             fetch(h, 0)
             turn_fetched(h, 0)
             turn_product(0, h)
-        for h in range(HALVES):
-            fetch(h, 1)
-        turn_fetched(0, 1)
+        fetch(0, 1)
         turn_product(0, 2)
+        scale_all(0)
         turn_product(1, 0)
-        for j in range(TURNED):
-            scale(0, j)
-            if j == 0:
-                warm_up(turned[j])
-            turn_one(1, 1, j)
+        stage(0)
+        turn_back(0)
+        fetch(1, 1, "prod0_2")
+        turn_fetched(1, 1)
         fetch(0, 2, "fetched0_1")
         turn_product(1, 1)
         turn_product(1, 2)
-        stage(0)
-        for j in range(TURNED):
-            add_back(0, j)
-        turn_back(0)
+        last_low = keep.tile([P, HALVES, SPLIT], F32, name="last_low")
+        fourth(last_low, 0, SPLIT)
+        finish_low(0)
+        last_high = keep.tile([P, HALVES, T - SPLIT], F32, name="last_high", tag="staged0")
+        fourth(last_high, SPLIT, T)
+        scale_all(1)
         fetch(1, 2, "prod0_2")
-        fourth(0, 0, T)
-        fourth(1, 0, T)
-        for j in range(TURNED):
-            scale(1, j)
-            for h in range(HALVES):
-                turn_one(h, 2, j)
-            add_back(1, j)
+        turn_fetched(1, 2)
         stage(1)
         turn_back(1)
-        for h in range(HALVES):
-            finish_low(h)
-        for j in range(TURNED):
-            scale(2, j)
-            add_back(2, j)
+        finish_low(1)
+        scale_all(2)
         out_view = out.rearrange("(h p) t -> p h t", p=P)
         for j in range(TURNED):
             total = keep.tile([P, HALVES, P], F32, name=f"high{j}")
-            lo = SPLIT + j * P
             nc.vector.tensor_add(
-                total[:], backs[j][:, 0:N].rearrange("p (h c) -> p h c", c=P), last[:, :, lo : lo + P]
+                total[:], backs[j][:, 0:N].rearrange("p (h c) -> p h c", c=P), last_high[:, :, j * P : (j + 1) * P]
             )
-            nc.sync.dma_start(out_view[:, :, lo : lo + P], total[:])
+            nc.sync.dma_start(out_view[:, :, SPLIT + j * P : SPLIT + (j + 1) * P], total[:])

@@ -264,18 +264,6 @@ def tile_moe_tk_lin_none_kernel(
         def turn_one(h, r, j):
             turn(turned[j][:, h * P : (h + 1) * P], fetched[h, r][:, j * P : (j + 1) * P], True, True)
 
-        def warm_up(bank):
-            for a in range(PASSES):
-                nc.tensor.matmul_mx(
-                    out=bank[:],
-                    lhsT=w_t[CHUNKS - 1][:, a, 0 : 2 * P].bitcast(FP4X4),
-                    lhsT_scale=w_sc[:, (E - GROUP) * PASSES + a, 0:P],
-                    rhs=words[a, CHUNKS - 1][:].bitcast(FP8X4),
-                    rhs_scale=(slot_bytes1 if a else slot_bytes)[:, SLOTS - CHUNK : SLOTS],
-                    start=True,
-                    stop=True,
-                )
-
         def finish_low(h):
             total = keep.tile([P, SPLIT], F32, name=f"low{h}")
             nc.vector.tensor_add(total[:], sums[h][:, 0:SPLIT], last_low[:, h, :])
@@ -292,7 +280,6 @@ def tile_moe_tk_lin_none_kernel(
                     turn_one(0, r + 1, j)
                 add_back(r, j)
 
-        warm_up(backs[-1])
         for h in range(HALVES):
             for r in range(EARLY):
                 product(h, r)

@@ -31,6 +31,8 @@ CHUNKS = SLOTS // CHUNK
 RAISED = 4
 SCALE_ROWS = 100
 RING = 4
+LONG = 2 * CHUNK
+WINDOW = 2 * T
 BANKS = 8
 
 LOADS = (((0, 256), (256, 512), (512, 640), (640, 768)), ((0, 256), (256, 512), (512, 768)))
@@ -55,7 +57,7 @@ def tile_moe_tk_lin_none_kernel(
         pos_t = [lists.tile([P, T // 16], U16, name=f"pos{r}_t") for r in range(TOP)]
 
         w_sc = keep.tile([P, E * PASSES, N], U8, name="w_sc", align_bytes=64)
-        tok_bytes = keep.tile([P, T], U8, name="tok_bytes", align_bytes=64)
+        tok_bytes = keep.tile([P, WINDOW], U8, name="tok_bytes", align_bytes=64)
         slot_bytes = keep.tile([P, SLOTS], U8, name="slot_bytes", align_bytes=64)
         slot_bytes1 = keep.tile([P, SLOTS], U8, name="slot_bytes1", align_bytes=64)
         ident = keep.tile([P, P], F32, name="ident")
@@ -68,7 +70,7 @@ def tile_moe_tk_lin_none_kernel(
         raw = {}
         for a in range(PASSES):
             for lo, hi in LOADS[a]:
-                tile = keep.tile([P, PACK, hi - lo], F32, name=f"raw{a}_{lo}")
+                tile = keep.tile([P, PACK, hi - lo], F32, name=f"raw{a}_{lo}", align_bytes=64)
                 nc.sync.dma_start(tile[:], x_view[a][:, :, lo:hi])
                 raw[a, lo] = tile
             if a == 0:
@@ -97,7 +99,7 @@ def tile_moe_tk_lin_none_kernel(
             nc.sync.dma_start(gate_t[r][:], gate[r, 0:P, 0 : SPLIT if r < EARLY else T])
 
         grouped = [keep.tile([P, T, PACK], BF16, name=f"grouped{a}", align_bytes=64) for a in range(PASSES)]
-        codes = [keep.tile([P, T], U32, name=f"codes{a}", align_bytes=64) for a in range(PASSES)]
+        codes = [keep.tile([P, WINDOW if a == 0 else T], U32, name=f"codes{a}", align_bytes=64) for a in range(PASSES)]
         words = {}
         y = [keep.tile([P, SLOTS], F32, name=f"y{h}") for h in range(HALVES)]
         banks = [psum.tile([P, CHUNK], F32, name=f"bank{i}") for i in range(BANKS)]
@@ -129,8 +131,14 @@ def tile_moe_tk_lin_none_kernel(
         def gather_chunk(a, g, tag=None):
             gather_words(a, g * CHUNK, (g + 1) * CHUNK, tag)
 
+        def gather_early(tile, g, count):
+            lo, hi = g * CHUNK, (g + count) * CHUNK
+            nc.vector.tensor_copy(tile[:], codes[0][:].indirect(offs_t[:, lo // 16 : hi // 16]))
+            for i in range(count):
+                words[0, g + i] = tile[:, i * CHUNK : (i + 1) * CHUNK]
+
         def gather_bytes(g):
-            lo, hi = g * CHUNK, (g + 1) * CHUNK
+            lo, hi = g * CHUNK, g * CHUNK + LONG
             nc.vector.tensor_copy(slot_bytes[:, lo:hi], tok_bytes[:].indirect(offs_t[:, lo // 16 : hi // 16]))
             nc.gpsimd.dma_start(
                 slot_bytes1[0:SCALE_ROWS, lo:hi].bitcast(I32),
@@ -163,13 +171,14 @@ def tile_moe_tk_lin_none_kernel(
 
         for j in range(TURNED):
             nc.tensor.transpose(banks[7][:, j * P : (j + 1) * P], gate_rows[:, j * P : (j + 1) * P], ident[:])
-        gate_cols = keep.tile([P, TURNED, EARLY], F32, name="gate_cols", tag=f"raw1_{LOADS[1][-1][0]}")
+        gate_cols = keep.tile([P, TURNED, EARLY], F32, name="gate_cols", tag=f"raw1_{LOADS[1][-2][0]}", align_bytes=64)
         nc.scalar.copy(gate_cols[:], banks[7][:, 0 : TURNED * P].rearrange("p (j c) -> p j c", c=P)[:, :, 0:EARLY])
 
-        for g in range(RING):
-            gather_chunk(0, g)
+        for g in (0, 2):
+            gather_early(keep.tile([P, LONG], U32, name=f"early{g}", align_bytes=64), g, 2)
         quantise(1, 0, 512)
         quantise(1, 512, T)
+        gather_early(keep.tile([P, CHUNK], U32, name="early4", tag=f"raw1_{LOADS[1][-1][0]}", align_bytes=64), 4, 1)
 
         def first_pass(g):
             one_pass(0, g * GROUP, GROUP, g % 4)
@@ -180,19 +189,16 @@ def tile_moe_tk_lin_none_kernel(
             for h in range(HALVES):
                 empty(nc.scalar.copy, h, g * GROUP, GROUP, g % 4)
 
-        for g in range(3):
+        for g in (0, 2):
             gather_bytes(g)
             first_pass(g)
+            first_pass(g + 1)
         second_pass(0)
-        gather_bytes(3)
-        first_pass(3)
-        second_pass(1)
         gather_bytes(4)
-        gather_bytes(5)
+        second_pass(1)
+        first_pass(4)
         second_pass(2)
         second_pass(3)
-        gather_chunk(0, 4)
-        first_pass(4)
         second_pass(4)
         gather_chunk(0, 5, "words1")
         pieces = ((E - 4, 2, 1), (E - 2, 1, 2), (E - 1, 1, 3))

@@ -85,6 +85,8 @@ def tile_moe_tk_lin_none_kernel(
             nc.gpsimd.dma_start(
                 w_sc[r:P:32].rearrange("q i n -> q (i n)").bitcast(I32), landed[4 + 8 * r : P : 32].bitcast(I32)
             )
+        for r, pos in enumerate((pos1, pos2, pos3, pos4)):
+            nc.sync.dma_start(pos_t[r][:], pos)
         w_view = w_words.bitcast(I32).rearrange("e a p c -> p (e a) c")
         w_t = []
         for g in range(CHUNKS):
@@ -92,14 +94,13 @@ def tile_moe_tk_lin_none_kernel(
             tile = tile[:].rearrange("p (i c) -> p i c", c=W_BYTES)
             nc.sync.dma_start(tile.bitcast(I32), w_view[:, g * GROUP * PASSES : (g + 1) * GROUP * PASSES])
             w_t.append(tile)
-        for r, pos in enumerate((pos1, pos2, pos3, pos4)):
-            nc.sync.dma_start(pos_t[r][:], pos)
-        gate_t = [keep.tile([P, SPLIT if r < EARLY else T], F32, name=f"gate{r}") for r in range(TOP)]
-        for r in range(TOP):
-            nc.sync.dma_start(gate_t[r][:], gate[r, 0:P, 0 : SPLIT if r < EARLY else T])
+        gate_low = keep.tile([P, TOP, SPLIT], F32, name="gate_low")
+        nc.sync.dma_start(gate_low[:], gate[:, 0:P, 0:SPLIT].rearrange("r p t -> p r t"))
+        gate_high = keep.tile([P, T - SPLIT], F32, name="gate_high")
+        nc.sync.dma_start(gate_high[:], gate[EARLY, 0:P, SPLIT:T])
 
         grouped = [keep.tile([P, T, PACK], BF16, name=f"grouped{a}", align_bytes=64) for a in range(PASSES)]
-        codes = [keep.tile([P, WINDOW if a == 0 else T], U32, name=f"codes{a}", align_bytes=64) for a in range(PASSES)]
+        codes = [keep.tile([P, T], U32, name=f"codes{a}", align_bytes=64) for a in range(PASSES)]
         words = {}
         y = [keep.tile([P, SLOTS], F32, name=f"y{h}") for h in range(HALVES)]
         banks = [psum.tile([P, CHUNK], F32, name=f"bank{i}") for i in range(BANKS)]
@@ -140,7 +141,7 @@ def tile_moe_tk_lin_none_kernel(
         def gather_bytes(g):
             lo, hi = g * CHUNK, g * CHUNK + LONG
             nc.vector.tensor_copy(slot_bytes[:, lo:hi], tok_bytes[:].indirect(offs_t[:, lo // 16 : hi // 16]))
-            nc.gpsimd.dma_start(
+            nc.scalar.dma_start(
                 slot_bytes1[0:SCALE_ROWS, lo:hi].bitcast(I32),
                 slot_bytes[RAISED : RAISED + SCALE_ROWS, lo:hi].bitcast(I32),
             )
@@ -174,8 +175,8 @@ def tile_moe_tk_lin_none_kernel(
         gate_cols = keep.tile([P, TURNED, EARLY], F32, name="gate_cols", tag=f"raw1_{LOADS[1][-2][0]}", align_bytes=64)
         nc.scalar.copy(gate_cols[:], banks[7][:, 0 : TURNED * P].rearrange("p (j c) -> p j c", c=P)[:, :, 0:EARLY])
 
-        for g in (0, 2):
-            gather_early(keep.tile([P, LONG], U32, name=f"early{g}", align_bytes=64), g, 2)
+        for g in range(4):
+            gather_early(keep.tile([P, CHUNK], U32, name=f"early{g}", align_bytes=64), g, 1)
         quantise(1, 0, 512)
         quantise(1, 512, T)
         gather_early(keep.tile([P, CHUNK], U32, name="early4", tag=f"raw1_{LOADS[1][-1][0]}", align_bytes=64), 4, 1)
@@ -225,7 +226,7 @@ def tile_moe_tk_lin_none_kernel(
 
         def product(h, r):
             prods[h, r] = keep.tile([P, SPLIT], F32, name=f"prod{h}_{r}", tag=f"prod{h}_{r}")
-            nc.vector.tensor_tensor(prods[h, r][:], window(h, r, 0, SPLIT), gate_t[r][:, 0:SPLIT], MULT)
+            nc.vector.tensor_tensor(prods[h, r][:], window(h, r, 0, SPLIT), gate_low[:, r, :], MULT)
 
         def turn_product(h, r):
             for c in range(0, SPLIT, P):
@@ -275,9 +276,9 @@ def tile_moe_tk_lin_none_kernel(
             nc.vector.tensor_add(total[:], sums[h][:, 0:SPLIT], last_low[:, h, :])
             nc.sync.dma_start(out[h * P : (h + 1) * P, 0:SPLIT], total[:])
 
-        def fourth(tile, lo, hi):
+        def fourth(tile, lo, hi, weight):
             for h in range(HALVES):
-                nc.vector.tensor_tensor(tile[:, h, :], window(h, EARLY, lo, hi), gate_t[EARLY][:, lo:hi], MULT)
+                nc.vector.tensor_tensor(tile[:, h, :], window(h, EARLY, lo, hi), weight, MULT)
 
         def scale_all(r):
             for j in range(TURNED):
@@ -305,10 +306,10 @@ def tile_moe_tk_lin_none_kernel(
         turn_product(1, 1)
         turn_product(1, 2)
         last_low = keep.tile([P, HALVES, SPLIT], F32, name="last_low")
-        fourth(last_low, 0, SPLIT)
+        fourth(last_low, 0, SPLIT, gate_low[:, EARLY, :])
         finish_low(0)
         last_high = keep.tile([P, HALVES, T - SPLIT], F32, name="last_high", tag="staged0")
-        fourth(last_high, SPLIT, T)
+        fourth(last_high, SPLIT, T, gate_high[:])
         scale_all(1)
         fetch(1, 2, "prod0_2")
         turn_fetched(1, 2)

@@ -35,8 +35,8 @@ LONG = 2 * CHUNK
 WINDOW = 2 * T
 BANKS = 8
 
-LOADS = (((0, 256), (256, 512), (512, 640), (640, 768)), ((0, 256), (256, 512), (512, 768)))
-SCALAR_SHARE = (96, 96, 48, 48)
+LOADS = (((0, 128), (128, 384), (384, 640), (640, 768)), ((0, 256), (256, 512), (512, 768)))
+SCALAR_SHARE = (64, 128, 112, 48)
 SPLIT = 384
 TURNED = (T - SPLIT) // P
 EARLY = TOP - 1

from contextlib import ExitStack

import concourse.mybir as mybir
from concourse.masks import make_identity

P = 128
PACK = 4
K, T, E, C, N = 1024, 768, 24, 128, 256
TOP = 4
PASSES = K // (P * PACK)
HALVES = N // P
SLOTS = E * C
FLOPS = 2 * K * N * SLOTS

F32 = mybir.dt.float32
BF16 = mybir.dt.bfloat16
I32 = mybir.dt.int32
U32 = mybir.dt.uint32
U16 = mybir.dt.uint16
U8 = mybir.dt.uint8
FP8X4 = mybir.dt.float8_e4m3fn_x4
FP4X4 = mybir.dt.float4_e2m1fn_x4
MULT = mybir.AluOpType.mult

COPY = mybir.ActivationFunctionType.Copy

W_BYTES = 2 * N
GROUP = 4
CHUNK = GROUP * C
CHUNKS = SLOTS // CHUNK
RAISED = 4
SCALE_ROWS = 100
RING = 4
LONG = 2 * CHUNK
WINDOW = 2 * T
BANKS = 8

LOADS = (((0, 128), (128, 384), (384, 640), (640, 768)), ((0, 256), (256, 512), (512, 768)))
SCALAR_SHARE = (64, 128, 112, 48)
SPLIT = 384
TURNED = (T - SPLIT) // P
EARLY = TOP - 1


def tile_moe_tk_lin_none_kernel(
    tc, xT, w_words, w_scales, gate, offs, pos1, pos2, pos3, pos4, out
):
    nc = tc.nc
    with ExitStack() as ctx:
        lists = ctx.enter_context(tc.tile_pool(name="lists", bufs=1))
        keep = ctx.enter_context(tc.tile_pool(name="keep", bufs=1))
        stream = ctx.enter_context(tc.tile_pool(name="stream", bufs=CHUNKS))
        ring = ctx.enter_context(tc.tile_pool(name="ring", bufs=RING))
        psum = ctx.enter_context(tc.psum_pool(name="psum", bufs=1))

        offs_t = lists.tile([P, SLOTS // 16], U16, name="offs_t")
        pos_t = [lists.tile([P, T // 16], U16, name=f"pos{r}_t") for r in range(TOP)]

        w_sc = keep.tile([P, E * PASSES, N], U8, name="w_sc", align_bytes=64)
        tok_bytes = keep.tile([P, WINDOW], U8, name="tok_bytes", align_bytes=64)
        slot_bytes = keep.tile([P, SLOTS], U8, name="slot_bytes", align_bytes=64)
        slot_bytes1 = keep.tile([P, SLOTS], U8, name="slot_bytes1", align_bytes=64)
        ident = keep.tile([P, P], F32, name="ident")
        make_identity(nc, ident[:])
        gate_rows = keep.tile([P, T - SPLIT], F32, name="gate_rows")
        nc.gpsimd.memset(gate_rows[:], 0.0)
        nc.gpsimd.dma_start(gate_rows[0:EARLY], gate[0:EARLY, 0, SPLIT:T])

        x_view = xT.rearrange("(a p j) t -> a p j t", a=PASSES, p=P, j=PACK)
        raw = {}
        for a in range(PASSES):
            for lo, hi in LOADS[a]:
                tile = keep.tile([P, PACK, hi - lo], F32, name=f"raw{a}_{lo}", align_bytes=64)
                nc.sync.dma_start(tile[:], x_view[a][:, :, lo:hi])
                raw[a, lo] = tile
            if a == 0:
                nc.sync.dma_start(offs_t[:], offs)
                landed = keep.tile([P, E * PASSES * N], U8, name="landed", align_bytes=64)
                nc.sync.dma_start(
                    landed[4:P:8].bitcast(I32).rearrange("q (i n) -> q i n", i=E * PASSES),
                    w_scales.bitcast(I32).rearrange("e a q n -> q (e a) n"),
                )

        for r in range(4):
            nc.gpsimd.dma_start(
                w_sc[r:P:32].rearrange("q i n -> q (i n)").bitcast(I32), landed[4 + 8 * r : P : 32].bitcast(I32)
            )
        for r, pos in enumerate((pos1, pos2, pos3, pos4)):
            nc.sync.dma_start(pos_t[r][:], pos)
        w_view = w_words.bitcast(I32).rearrange("e a p c -> p (e a) c")
        w_t = []
        for g in range(CHUNKS):
            tile = stream.tile([P, GROUP * PASSES * W_BYTES], U8, name=f"w{g}", tag="stream", align_bytes=64)
            tile = tile[:].rearrange("p (i c) -> p i c", c=W_BYTES)
            nc.sync.dma_start(tile.bitcast(I32), w_view[:, g * GROUP * PASSES : (g + 1) * GROUP * PASSES])
            w_t.append(tile)
        gate_low = keep.tile([P, TOP, SPLIT], F32, name="gate_low")
        nc.sync.dma_start(gate_low[:], gate[:, 0:P, 0:SPLIT].rearrange("r p t -> p r t"))
        gate_high = keep.tile([P, T - SPLIT], F32, name="gate_high")
        nc.sync.dma_start(gate_high[:], gate[EARLY, 0:P, SPLIT:T])

        grouped = [keep.tile([P, T, PACK], BF16, name=f"grouped{a}", align_bytes=64) for a in range(PASSES)]
        codes = [keep.tile([P, T], U32, name=f"codes{a}", align_bytes=64) for a in range(PASSES)]
        words = {}
        y = [keep.tile([P, SLOTS], F32, name=f"y{h}") for h in range(HALVES)]
        banks = [psum.tile([P, CHUNK], F32, name=f"bank{i}") for i in range(BANKS)]

        def scalar_move(dst, src):
            nc.scalar.activation(dst, src, COPY)

        def cast(engine_copy, a, load, lo, hi):
            engine_copy(
                grouped[a][:, lo:hi, :].rearrange("p (c i) j -> p c j i", i=PACK),
                raw[a, load][:, :, lo - load : hi - load].rearrange("p j (c i) -> p c j i", i=PACK),
            )

        def quantise(a, lo, hi):
            nc.vector.quantize_mx(
                out=codes[a][:, lo:hi].bitcast(FP8X4),
                scales=tok_bytes[RAISED * a : P, lo:hi],
                in_=grouped[a][:, lo:hi, :].rearrange("p w j -> p (w j)"),
            )

        def gather_words(a, lo, hi, tag=None):
            g = lo // CHUNK
            if lo == g * CHUNK:
                words[a, g] = ring.tile([P, CHUNK], U32, name=f"words{a}", tag=tag or f"words{a}", align_bytes=64)
            nc.vector.tensor_copy(
                words[a, g][:, lo - g * CHUNK : hi - g * CHUNK], codes[a][:].indirect(offs_t[:, lo // 16 : hi // 16])
            )

        def gather_chunk(a, g, tag=None):
            gather_words(a, g * CHUNK, (g + 1) * CHUNK, tag)

        def gather_early(tile, g, count):
            lo, hi = g * CHUNK, (g + count) * CHUNK
            nc.vector.tensor_copy(tile[:], codes[0][:].indirect(offs_t[:, lo // 16 : hi // 16]))
            for i in range(count):
                words[0, g + i] = tile[:, i * CHUNK : (i + 1) * CHUNK]

        def gather_bytes(g):
            lo, hi = g * CHUNK, g * CHUNK + LONG
            nc.vector.tensor_copy(slot_bytes[:, lo:hi], tok_bytes[:].indirect(offs_t[:, lo // 16 : hi // 16]))
            nc.scalar.dma_start(
                slot_bytes1[0:SCALE_ROWS, lo:hi].bitcast(I32),
                slot_bytes[RAISED : RAISED + SCALE_ROWS, lo:hi].bitcast(I32),
            )

        def one_pass(a, first, count, pair):
            for h in range(HALVES):
                for e in range(first, first + count):
                    i = (e % GROUP) * PASSES + a
                    nc.tensor.matmul_mx(
                        out=banks[2 * pair + h][:, (e - first) * C : (e - first + 1) * C],
                        lhsT=w_t[e // GROUP][:, i, 2 * P * h : 2 * P * (h + 1)].bitcast(FP4X4),
                        lhsT_scale=w_sc[:, e * PASSES + a, P * h : P * (h + 1)],
                        rhs=words[a, e // GROUP][:, (e % GROUP) * C : (e % GROUP + 1) * C].bitcast(FP8X4),
                        rhs_scale=(slot_bytes1 if a else slot_bytes)[:, e * C : (e + 1) * C],
                        start=(a == 0 and e == first),
                        stop=(a == PASSES - 1 and e == first + count - 1),
                    )

        def empty(engine_copy, h, first, count, pair):
            engine_copy(y[h][:, first * C : (first + count) * C], banks[2 * pair + h][:, 0 : count * C])

        for (lo, hi), share in zip(LOADS[0], SCALAR_SHARE):
            cast(scalar_move, 0, lo, lo, lo + share)
            cast(nc.vector.tensor_copy, 0, lo, lo + share, hi)
            quantise(0, lo, hi)
        for lo, hi in LOADS[1]:
            cast(scalar_move, 1, lo, lo, hi)

        for j in range(TURNED):
            nc.tensor.transpose(banks[7][:, j * P : (j + 1) * P], gate_rows[:, j * P : (j + 1) * P], ident[:])
        gate_cols = keep.tile([P, TURNED, EARLY], F32, name="gate_cols", tag=f"raw1_{LOADS[1][-2][0]}", align_bytes=64)
        nc.scalar.copy(gate_cols[:], banks[7][:, 0 : TURNED * P].rearrange("p (j c) -> p j c", c=P)[:, :, 0:EARLY])

        for g in range(4):
            gather_early(keep.tile([P, CHUNK], U32, name=f"early{g}", align_bytes=64), g, 1)
        quantise(1, 0, 512)
        quantise(1, 512, T)
        gather_early(keep.tile([P, CHUNK], U32, name="early4", tag=f"raw1_{LOADS[1][-1][0]}", align_bytes=64), 4, 1)

        def first_pass(g):
            one_pass(0, g * GROUP, GROUP, g % 4)

        def second_pass(g):
            gather_chunk(1, g)
            one_pass(1, g * GROUP, GROUP, g % 4)
            for h in range(HALVES):
                empty(nc.scalar.copy, h, g * GROUP, GROUP, g % 4)

        for g in (0, 2):
            gather_bytes(g)
            first_pass(g)
            first_pass(g + 1)
        second_pass(0)
        gather_bytes(4)
        second_pass(1)
        first_pass(4)
        second_pass(2)
        second_pass(3)
        second_pass(4)
        gather_chunk(0, 5, "words1")
        pieces = ((E - 4, 2, 1), (E - 2, 1, 2), (E - 1, 1, 3))
        for first, count, pair in pieces:
            one_pass(0, first, count, pair)
        for first, count, pair in pieces:
            gather_words(1, first * C, (first + count) * C)
            one_pass(1, first, count, pair)
            empty(nc.scalar.copy, 0, first, count, pair)
        for first, count, pair in pieces:
            empty(nc.scalar.copy if first == E - 1 else nc.vector.tensor_copy, 1, first, count, pair)

        def window(h, r, lo, hi):
            return y[h][:].indirect(pos_t[r][:, lo // 16 : hi // 16])

        def turn(target, source, start, stop):
            nc.tensor.matmul(target, lhsT=source, rhs=ident[:], is_transpose=True, start=start, stop=stop)

        turned = banks[0:TURNED]
        sums = banks[TURNED : TURNED + HALVES]
        backs = banks[TURNED + HALVES :]

        prods = {}

        def product(h, r):
            prods[h, r] = keep.tile([P, SPLIT], F32, name=f"prod{h}_{r}", tag=f"prod{h}_{r}")
            nc.vector.tensor_tensor(prods[h, r][:], window(h, r, 0, SPLIT), gate_low[:, r, :], MULT)

        def turn_product(h, r):
            for c in range(0, SPLIT, P):
                first, final = r == 0 and c == 0, r == EARLY - 1 and c == SPLIT - P
                turn(sums[h][:, c : c + P], prods[h, r][:, c : c + P], first, final)

        fetched = {}

        def fetch(h, r, tag=None):
            fetched[h, r] = keep.tile([P, T - SPLIT], F32, name=f"fetched{h}_{r}", tag=tag or f"fetched{h}_{r}")
            scalar_move(fetched[h, r][:], window(h, r, SPLIT, T))

        def turn_fetched(h, r):
            for j in range(TURNED):
                turn_one(h, r, j)

        scaled = {}

        def scale(r, j):
            scaled[r, j] = keep.tile([P, N], F32, name=f"scaled{r}_{j}")
            nc.scalar.activation(scaled[r, j][:], turned[j][:, 0:N], COPY, scale=gate_cols[:, j, r : r + 1])

        def add_back(r, j):
            for h in range(HALVES):
                turn(
                    backs[j][:, h * P : (h + 1) * P],
                    scaled[r, j][:, h * P : (h + 1) * P],
                    r == 0 and h == 0,
                    r == EARLY - 1 and h == HALVES - 1,
                )

        staged = {}

        def stage(h):
            staged[h] = keep.tile([P, SPLIT], F32, name=f"staged{h}", tag=f"staged{h}")
            nc.scalar.copy(staged[h][:], sums[h][:, 0:SPLIT])

        def turn_back(h):
            for c in range(0, SPLIT, P):
                turn(sums[h][:, c : c + P], staged[h][:, c : c + P], True, True)

        def turn_one(h, r, j):
            turn(turned[j][:, h * P : (h + 1) * P], fetched[h, r][:, j * P : (j + 1) * P], True, True)

        def finish_low(h):
            total = keep.tile([P, SPLIT], F32, name=f"low{h}")
            nc.vector.tensor_add(total[:], sums[h][:, 0:SPLIT], last_low[:, h, :])
            nc.sync.dma_start(out[h * P : (h + 1) * P, 0:SPLIT], total[:])

        def fourth(tile, lo, hi, weight):
            for h in range(HALVES):
                nc.vector.tensor_tensor(tile[:, h, :], window(h, EARLY, lo, hi), weight, MULT)

        def scale_all(r):
            for j in range(TURNED):
                scale(r, j)
                if r + 1 < EARLY:
                    turn_one(0, r + 1, j)
                add_back(r, j)

        for h in range(HALVES):
            for r in range(EARLY):
                product(h, r)
        for h in range(HALVES):
            fetch(h, 0)
            turn_fetched(h, 0)
            turn_product(0, h)
        fetch(0, 1)
        turn_product(0, 2)
        scale_all(0)
        turn_product(1, 0)
        stage(0)
        turn_back(0)
        fetch(1, 1, "prod0_2")
        turn_fetched(1, 1)
        fetch(0, 2, "fetched0_1")
        turn_product(1, 1)
        turn_product(1, 2)
        last_low = keep.tile([P, HALVES, SPLIT], F32, name="last_low")
        fourth(last_low, 0, SPLIT, gate_low[:, EARLY, :])
        finish_low(0)
        last_high = keep.tile([P, HALVES, T - SPLIT], F32, name="last_high", tag="staged0")
        fourth(last_high, SPLIT, T, gate_high[:])
        scale_all(1)
        fetch(1, 2, "prod0_2")
        turn_fetched(1, 2)
        stage(1)
        turn_back(1)
        finish_low(1)
        scale_all(2)
        out_view = out.rearrange("(h p) t -> p h t", p=P)
        for j in range(TURNED):
            total = keep.tile([P, HALVES, P], F32, name=f"high{j}")
            nc.vector.tensor_add(
                total[:], backs[j][:, 0:N].rearrange("p (h c) -> p h c", c=P), last_high[:, :, j * P : (j + 1) * P]
            )
            nc.sync.dma_start(out_view[:, :, SPLIT + j * P : SPLIT + (j + 1) * P], total[:])
